import numpy as np
import ml_dtypes


def mxq(x, axis, fmt="e4m3"):
    dtype, down = {"e4m3": (ml_dtypes.float8_e4m3fn, 7), "e5m2": (ml_dtypes.float8_e5m2, 14)}[fmt]
    v = np.moveaxis(np.asarray(x, np.float32).astype(ml_dtypes.bfloat16).astype(np.float64), axis, -1)
    blocks = v.reshape(v.shape[:-1] + (-1, 32))
    amax = np.abs(blocks).max(-1, keepdims=True)
    byte = np.maximum(np.where(amax > 0, np.frexp(amax)[1] - 1 + 127, 0) - down, 1)
    scale = np.exp2(byte - 127.0)
    codes = (blocks / scale).astype(np.float32).astype(dtype).astype(np.float64)
    return np.moveaxis((codes * scale).reshape(v.shape), -1, axis)


WIDE = False


def mx_kscale(k):
    if not WIDE:
        return np.ones(k)
    levels = np.array([10, -10, 5, -5, 0])
    if k % 512:
        return np.exp2(np.random.permutation(np.resize(levels, k // 32))).repeat(32)
    a = np.empty((k // 512, 16))
    for p in range(k // 512):
        a[p, :8] = np.random.permutation(np.resize(levels, 8))
        for g in range(8):
            far = levels[np.abs(levels - a[p, g]) >= 10]
            a[p, g + 8] = far[np.random.randint(len(far))]
    return np.exp2(a.ravel()).repeat(32)


def f64(x):
    return np.asarray(x).astype(np.float64)


def striped(idx):
    return np.tile(idx.reshape(-1, 16).T, (8, 1)).astype(np.uint16)


def unstriped(offs):
    return offs[:16].T.reshape(-1).astype(np.int64)


def pack_weight(w):
    k, n = w.shape
    w = f64(np.asarray(w, np.float32).astype(ml_dtypes.bfloat16)).reshape(k // 32, 32, n)
    amax = np.abs(w).max(1)
    byte = np.clip(np.where(amax > 0, np.frexp(amax)[1] - 1 + 127 - 7, 1), 1, 254)
    scaled = (w * np.exp2(127.0 - byte)[:, None, :]).reshape(k, n).astype(np.float32)
    words = np.ascontiguousarray(scaled.reshape(k // 512, 128, 4, n).transpose(0, 1, 3, 2)).astype(ml_dtypes.float8_e4m3fn).view(np.uint8)
    return words, np.ascontiguousarray(byte.astype(np.uint8).reshape(k // 512, 16, n))


def unpack_weight(words, scales):
    g, p, n, _ = words.shape
    vals = np.ascontiguousarray(words).view(ml_dtypes.float8_e4m3fn).astype(np.float64) * np.repeat(np.exp2(scales.astype(np.float64) - 127.0), 8, axis=1)[..., None]
    return vals.transpose(0, 1, 3, 2).reshape(g * 512, n)


K, T, S, N = 1024, 2048, 1024, 256
P = 2 ** 7


def setup_inputs():
    n = np.random.standard_normal
    s = mx_kscale(K)[:, None]
    packed_w1 = pack_weight(n((K, N)) / np.sqrt(K) / s)
    return {
        "xT": (n((K, T)) * s).astype(np.float32),
        "zp": np.tile(np.random.uniform(-0.6, 0.6, T), (P, 1)).astype(np.float32),
        "csum": n((N, 1)).astype(np.float32),
        "w1_words": packed_w1[0],
        "w1_scales": packed_w1[1],
        "offs": striped(np.random.permutation(T)[:S]),
    }


def reference(xT, zp, csum, w1_words, w1_scales, offs):
    xq = mxq(f64(xT)[:, unstriped(offs)], 0, "e4m3")
    y = unpack_weight(w1_words, w1_scales).T @ xq
    zg = f64(zp)[:1][:, unstriped(offs)]
    return y - (f64(csum) * zg)

@@ -1,0 +1,183 @@
+from contextlib import ExitStack
+
+import concourse.mybir as mybir
+from concourse.masks import make_identity
+
+K, T, S, N = 1024, 2048, 1024, 256
+FLOPS = 2 * K * S * N
+BYTES = 4 * K * T + 4 * T + 4 * N + K * N + K * N // 32 + 2 * 128 * S // 16 + 4 * N * S
+
+F32 = mybir.dt.float32
+BF16 = mybir.dt.bfloat16
+U32 = mybir.dt.uint32
+I32 = mybir.dt.int32
+U16 = mybir.dt.uint16
+U8 = mybir.dt.uint8
+FP8X4 = mybir.dt.float8_e4m3fn_x4
+MULT = mybir.AluOpType.mult
+ADD = mybir.AluOpType.add
+
+P = 128
+PASSES = K // (4 * P)
+BLOCKS = N // P
+CHUNK = 256
+CHUNKS = S // CHUNK
+LIST_COLS = CHUNK // 16
+ZP_COLS = T // P
+LOAD_EDGES = [0, 1024, 2048]
+LAST_LOAD_EDGES = [0, 1024, 1536, 2048]
+
+
+def tile_picked_zeropt_none_l_kernel(tc, xT, zp, csum, w1_words, w1_scales, offs, out):
+    nc = tc.nc
+    with ExitStack() as ctx:
+        keep = ctx.enter_context(tc.tile_pool(name="keep", bufs=1))
+        psum = ctx.enter_context(tc.psum_pool(name="psum", bufs=1))
+
+        offsets = keep.tile([P, S // 16], U16, name="offsets")
+        zp_rows = keep.tile([P, ZP_COLS], F32, name="zp_rows")
+        nc.scalar.dma_start(zp_rows[:], zp[0, :].rearrange("(n m) -> n m", m=ZP_COLS))
+
+        csum_cols = keep.tile([P, BLOCKS], F32, name="csum_cols")
+        with nc.allow_non_contiguous_dma(reason="one value a channel"):
+            nc.scalar.dma_start(csum_cols[:], csum.rearrange("(b p) o -> p (b o)", p=P))
+
+        x_rows = xT.rearrange("(z p h e) t -> z h p e t", z=PASSES, p=P, h=2, e=2)
+        raw = {}
+
+        def load_pair(z, h, edges):
+            for lo, hi in zip(edges[:-1], edges[1:]):
+                piece = keep.tile([P, 2, hi - lo], F32, name=f"raw_{z}_{h}_{lo}")
+                nc.sync.dma_start(piece[:], x_rows[z, h, :, :, lo:hi])
+                raw[z, h, lo] = piece
+
+        w_scales = keep.tile([P, N], U8, name="w_scales", align_bytes=64)
+        nc.gpsimd.memset(w_scales[:].bitcast(I32), 0)
+        ident = keep.tile([P, P], F32, name="ident")
+        make_identity(nc, ident[:])
+
+        load_pair(0, 0, LOAD_EDGES)
+        nc.sync.dma_start(offsets[:], offs)
+        load_pair(0, 1, LOAD_EDGES)
+        for q in range(4):
+            nc.scalar.dma_start(
+                w_scales[32 * q : 32 * q + 4 * PASSES, :].bitcast(I32),
+                w1_scales[:, 4 * q : 4 * q + 4, :].bitcast(I32),
+            )
+        load_pair(1, 0, LOAD_EDGES)
+        load_pair(1, 1, LAST_LOAD_EDGES)
+        w_words = keep.tile([P, PASSES, N], U32, name="w_words", align_bytes=64)
+        nc.sync.dma_start(
+            w_words[:].bitcast(I32),
+            w1_words.rearrange("z p n t -> p z (n t)").bitcast(I32),
+        )
+
+        neg_csum = keep.tile([P, BLOCKS], F32, name="neg_csum")
+        nc.gpsimd.tensor_scalar(neg_csum[:], csum_cols[:], -1.0, 0.0, MULT, ADD)
+
+        zp_window = keep.tile([P, T], F32, name="zp_window")
+        zp_view = zp_window[:].rearrange("p (n m) -> p n m", m=ZP_COLS)
+        for q in range(ZP_COLS // 4):
+            spread = psum.tile([P, 4, P], F32, name=f"spread_{q}", tag=f"bank_{q}")
+            for i in range(4):
+                m = 4 * q + i
+                nc.tensor.transpose(spread[:, i, :], zp_rows[:, m : m + 1].to_broadcast([P, P]), ident[:])
+            nc.vector.tensor_copy(zp_view[:, :, 4 * q : 4 * q + 4], spread[:].rearrange("p i n -> p n i"))
+        zp_picked = keep.tile([P, S], F32, name="zp_picked")
+        nc.vector.tensor_copy(zp_picked[:], zp_window[:].indirect(offsets[:]))
+
+        def cast(engine_copy, window, z, h, lo, a, b):
+            engine_copy(window[:, a:b, :], raw[z, h, lo][:, :, a - lo : b - lo].rearrange("p e c -> p c e"))
+
+        def pair_words(window):
+            return window[:].rearrange("p c e -> p (c e)").bitcast(U32)
+
+        windows = {}
+        for z in range(PASSES):
+            for h in range(2):
+                windows[z, h] = keep.tile([P, T, 2], BF16, name=f"window_{z}_{h}")
+
+        sums = {}
+        for c in range(CHUNKS):
+            for b in range(BLOCKS):
+                sums[c, b] = psum.tile([P, CHUNK], F32, name=f"sums_{c}_{b}", tag=f"bank_{(4 + BLOCKS * c + b) % 8}")
+
+        def multiply(z, c, codes, scales):
+            for b in range(BLOCKS):
+                cols = slice(b * P, (b + 1) * P)
+                nc.tensor.matmul_mx(
+                    out=sums[c, b][:],
+                    lhsT=w_words[:, z, cols].bitcast(FP8X4),
+                    lhsT_scale=w_scales[4 * z : P, cols],
+                    rhs=codes.bitcast(FP8X4),
+                    rhs_scale=scales,
+                    start=(z == 0),
+                    stop=(z == PASSES - 1),
+                )
+
+        picked0 = keep.tile([P, 2, S], U32, name="picked0")
+        for h in range(2):
+            cast(nc.scalar.copy, windows[0, h], 0, h, 0, 0, 1024)
+            cast(nc.scalar.copy, windows[0, h], 0, h, 1024, 1024, 1408)
+            cast(nc.vector.tensor_copy, windows[0, h], 0, h, 1024, 1408, 2048)
+            nc.vector.tensor_copy(picked0[:, h, :], pair_words(windows[0, h]).indirect(offsets[:]))
+        woven0 = keep.tile([P, S, 2], I32, name="woven0", align_bytes=64)
+        nc.vector.tensor_copy(woven0[:], picked0[:].bitcast(I32).rearrange("p h s -> p s h"))
+        codes0 = keep.tile([P, S], U32, name="codes0", align_bytes=64)
+        scales0 = keep.tile([P, S], U8, name="scales0", align_bytes=64)
+        nc.vector.quantize_mx(
+            out=codes0[:].bitcast(FP8X4), scales=scales0[:], in_=woven0[:].rearrange("p s h -> p (s h)").bitcast(BF16)
+        )
+
+        picked1 = [keep.tile([P, 2, CHUNK], U32, name=f"picked1_{c}") for c in range(CHUNKS)]
+
+        def gather1(h, c):
+            nc.vector.tensor_copy(
+                picked1[c][:, h, :], pair_words(windows[1, h]).indirect(offsets[:, c * LIST_COLS : (c + 1) * LIST_COLS])
+            )
+
+        cast(nc.scalar.copy, windows[1, 0], 1, 0, 0, 0, 1024)
+        cast(nc.scalar.copy, windows[1, 0], 1, 0, 1024, 1024, 1728)
+        cast(nc.vector.tensor_copy, windows[1, 0], 1, 0, 1024, 1728, 2048)
+        for c in range(CHUNKS):
+            gather1(0, c)
+        cast(nc.scalar.copy, windows[1, 1], 1, 1, 0, 0, 1024)
+        cast(nc.vector.tensor_copy, windows[1, 1], 1, 1, 1024, 1024, 1536)
+        cast(nc.scalar.copy, windows[1, 1], 1, 1, 1536, 1536, 1792)
+        cast(nc.vector.tensor_copy, windows[1, 1], 1, 1, 1536, 1792, 2048)
+
+        for c in range(CHUNKS):
+            multiply(0, c, codes0[:, c * CHUNK : (c + 1) * CHUNK], scales0[:, c * CHUNK : (c + 1) * CHUNK])
+
+        woven1 = [keep.tile([P, CHUNK, 2], U32, name=f"woven1_{c}", align_bytes=64) for c in range(CHUNKS)]
+        codes1 = [keep.tile([P, CHUNK], U32, name=f"codes1_{c}", align_bytes=64) for c in range(CHUNKS)]
+        scales1 = [keep.tile([P, CHUNK], U8, name=f"scales1_{c}", align_bytes=64) for c in range(CHUNKS)]
+
+        def pick(c):
+            gather1(1, c)
+            nc.scalar.copy(woven1[c][:], picked1[c][:].rearrange("p h s -> p s h"))
+
+        def quantise(c):
+            nc.vector.quantize_mx(
+                out=codes1[c][:].bitcast(FP8X4),
+                scales=scales1[c][:],
+                in_=woven1[c][:].rearrange("p s h -> p (s h)").bitcast(BF16),
+            )
+            multiply(1, c, codes1[c][:], scales1[c][:])
+
+        def finish(c):
+            cols = slice(c * CHUNK, (c + 1) * CHUNK)
+            for b in range(BLOCKS):
+                result = keep.tile([P, CHUNK], F32, name=f"result_{c}_{b}")
+                nc.vector.scalar_tensor_tensor(
+                    result[:], zp_picked[:, cols], neg_csum[:, b : b + 1], sums[c, b][:], MULT, ADD
+                )
+                nc.sync.dma_start(out[b * P : (b + 1) * P, cols], result[:])
+
+        for step in range(CHUNKS + 2):
+            if step < CHUNKS:
+                pick(step)
+            if 1 <= step <= CHUNKS:
+                quantise(step - 1)
+            if step >= 2:
+                finish(step - 2)

@@ -24,8 +24,10 @@ CHUNK = 256
 CHUNKS = S // CHUNK
 LIST_COLS = CHUNK // 16
 ZP_COLS = T // P
-LOAD_EDGES = [0, 1024, 2048]
-LAST_LOAD_EDGES = [0, 1024, 1536, 2048]
+HALF = T // 2
+PAIRS = [(z, h) for z in range(PASSES) for h in range(2)]
+PIECES = [[(HALF, T), (0, HALF)]] * 3 + [[(HALF, T), (0, HALF // 2), (HALF // 2, HALF)]]
+VECTOR_TOKENS = [0, 640, 0, 640]
 
 
 def tile_picked_zeropt_none_l_kernel(tc, xT, zp, csum, w1_words, w1_scales, offs, out):
@@ -36,36 +38,37 @@ def tile_picked_zeropt_none_l_kernel(tc, xT, zp, csum, w1_words, w1_scales, offs
 
         offsets = keep.tile([P, S // 16], U16, name="offsets")
         zp_rows = keep.tile([P, ZP_COLS], F32, name="zp_rows")
-        nc.scalar.dma_start(zp_rows[:], zp[0, :].rearrange("(n m) -> n m", m=ZP_COLS))
+        nc.sync.dma_start(zp_rows[:], zp[0, :].rearrange("(n m) -> n m", m=ZP_COLS))
 
-        csum_cols = keep.tile([P, BLOCKS], F32, name="csum_cols")
-        with nc.allow_non_contiguous_dma(reason="one value a channel"):
-            nc.scalar.dma_start(csum_cols[:], csum.rearrange("(b p) o -> p (b o)", p=P))
+        nc.sync.dma_start(offsets[:], offs)
 
         x_rows = xT.rearrange("(z p h e) t -> z h p e t", z=PASSES, p=P, h=2, e=2)
         raw = {}
 
-        def load_pair(z, h, edges):
-            for lo, hi in zip(edges[:-1], edges[1:]):
-                piece = keep.tile([P, 2, hi - lo], F32, name=f"raw_{z}_{h}_{lo}")
+        def load_pair(i):
+            z, h = PAIRS[i]
+            for lo, hi in PIECES[i]:
+                piece = keep.tile([P, 2, hi - lo], F32, name=f"raw_{i}_{lo}")
                 nc.sync.dma_start(piece[:], x_rows[z, h, :, :, lo:hi])
-                raw[z, h, lo] = piece
+                raw[i, lo] = piece
 
         w_scales = keep.tile([P, N], U8, name="w_scales", align_bytes=64)
         nc.gpsimd.memset(w_scales[:].bitcast(I32), 0)
         ident = keep.tile([P, P], F32, name="ident")
         make_identity(nc, ident[:])
 
-        load_pair(0, 0, LOAD_EDGES)
-        nc.sync.dma_start(offsets[:], offs)
-        load_pair(0, 1, LOAD_EDGES)
+        load_pair(0)
+        csum_cols = keep.tile([P, BLOCKS], F32, name="csum_cols")
+        with nc.allow_non_contiguous_dma(reason="one value a channel"):
+            nc.sync.dma_start(csum_cols[:], csum.rearrange("(b p) o -> p (b o)", p=P))
         for q in range(4):
-            nc.scalar.dma_start(
+            nc.sync.dma_start(
                 w_scales[32 * q : 32 * q + 4 * PASSES, :].bitcast(I32),
                 w1_scales[:, 4 * q : 4 * q + 4, :].bitcast(I32),
             )
-        load_pair(1, 0, LOAD_EDGES)
-        load_pair(1, 1, LAST_LOAD_EDGES)
+        load_pair(1)
+        load_pair(2)
+        load_pair(3)
         w_words = keep.tile([P, PASSES, N], U32, name="w_words", align_bytes=64)
         nc.sync.dma_start(
             w_words[:].bitcast(I32),
@@ -75,7 +78,7 @@ def tile_picked_zeropt_none_l_kernel(tc, xT, zp, csum, w1_words, w1_scales, offs
         neg_csum = keep.tile([P, BLOCKS], F32, name="neg_csum")
         nc.gpsimd.tensor_scalar(neg_csum[:], csum_cols[:], -1.0, 0.0, MULT, ADD)
 
-        zp_window = keep.tile([P, T], F32, name="zp_window")
+        zp_window = keep.tile([P, T], F32, name="zp_window", tag="zp_window_then_picked0")
         zp_view = zp_window[:].rearrange("p (n m) -> p n m", m=ZP_COLS)
         for q in range(ZP_COLS // 4):
             spread = psum.tile([P, 4, P], F32, name=f"spread_{q}", tag=f"bank_{q}")
@@ -86,16 +89,21 @@ def tile_picked_zeropt_none_l_kernel(tc, xT, zp, csum, w1_words, w1_scales, offs
         zp_picked = keep.tile([P, S], F32, name="zp_picked")
         nc.vector.tensor_copy(zp_picked[:], zp_window[:].indirect(offsets[:]))
 
-        def cast(engine_copy, window, z, h, lo, a, b):
-            engine_copy(window[:, a:b, :], raw[z, h, lo][:, :, a - lo : b - lo].rearrange("p e c -> p c e"))
+        starts = [i * T - sum(VECTOR_TOKENS[: i + 1]) for i in range(len(PAIRS))]
+        pairs = keep.tile([P, 2 * (starts[-1] + T)], BF16, name="pairs")
 
-        def pair_words(window):
-            return window[:].rearrange("p c e -> p (c e)").bitcast(U32)
+        def cast(i):
+            for lo, hi in PIECES[i]:
+                cut = min(max(VECTOR_TOKENS[i], lo), hi)
+                for copy, a, b in ((nc.scalar.copy, cut, hi), (nc.vector.tensor_copy, lo, cut)):
+                    if a < b:
+                        copy(
+                            pairs[:, 2 * (starts[i] + a) : 2 * (starts[i] + b)].rearrange("p (c e) -> p c e", e=2),
+                            raw[i, lo][:, :, a - lo : b - lo].rearrange("p e c -> p c e"),
+                        )
 
-        windows = {}
-        for z in range(PASSES):
-            for h in range(2):
-                windows[z, h] = keep.tile([P, T, 2], BF16, name=f"window_{z}_{h}")
+        def window(i):
+            return pairs[:, 2 * starts[i] : 2 * (starts[i] + T)].bitcast(U32)
 
         sums = {}
         for c in range(CHUNKS):
@@ -115,12 +123,10 @@ def tile_picked_zeropt_none_l_kernel(tc, xT, zp, csum, w1_words, w1_scales, offs
                     stop=(z == PASSES - 1),
                 )
 
-        picked0 = keep.tile([P, 2, S], U32, name="picked0")
+        picked0 = keep.tile([P, 2, S], U32, name="picked0", tag="zp_window_then_picked0")
         for h in range(2):
-            cast(nc.scalar.copy, windows[0, h], 0, h, 0, 0, 1024)
-            cast(nc.scalar.copy, windows[0, h], 0, h, 1024, 1024, 1408)
-            cast(nc.vector.tensor_copy, windows[0, h], 0, h, 1024, 1408, 2048)
-            nc.vector.tensor_copy(picked0[:, h, :], pair_words(windows[0, h]).indirect(offsets[:]))
+            cast(h)
+            nc.vector.tensor_copy(picked0[:, h, :], window(h).indirect(offsets[:]))
         woven0 = keep.tile([P, S, 2], I32, name="woven0", align_bytes=64)
         nc.vector.tensor_copy(woven0[:], picked0[:].bitcast(I32).rearrange("p h s -> p s h"))
         codes0 = keep.tile([P, S], U32, name="codes0", align_bytes=64)
@@ -133,18 +139,13 @@ def tile_picked_zeropt_none_l_kernel(tc, xT, zp, csum, w1_words, w1_scales, offs
 
         def gather1(h, c):
             nc.vector.tensor_copy(
-                picked1[c][:, h, :], pair_words(windows[1, h]).indirect(offsets[:, c * LIST_COLS : (c + 1) * LIST_COLS])
+                picked1[c][:, h, :], window(2 + h).indirect(offsets[:, c * LIST_COLS : (c + 1) * LIST_COLS])
             )
 
-        cast(nc.scalar.copy, windows[1, 0], 1, 0, 0, 0, 1024)
-        cast(nc.scalar.copy, windows[1, 0], 1, 0, 1024, 1024, 1728)
-        cast(nc.vector.tensor_copy, windows[1, 0], 1, 0, 1024, 1728, 2048)
+        cast(2)
         for c in range(CHUNKS):
             gather1(0, c)
-        cast(nc.scalar.copy, windows[1, 1], 1, 1, 0, 0, 1024)
-        cast(nc.vector.tensor_copy, windows[1, 1], 1, 1, 1024, 1024, 1536)
-        cast(nc.scalar.copy, windows[1, 1], 1, 1, 1536, 1536, 1792)
-        cast(nc.vector.tensor_copy, windows[1, 1], 1, 1, 1536, 1792, 2048)
+        cast(3)
 
         for c in range(CHUNKS):
             multiply(0, c, codes0[:, c * CHUNK : (c + 1) * CHUNK], scales0[:, c * CHUNK : (c + 1) * CHUNK])

@@ -20,14 +20,19 @@ ADD = mybir.AluOpType.add
 P = 128
 PASSES = K // (4 * P)
 BLOCKS = N // P
-CHUNK = 256
-CHUNKS = S // CHUNK
-LIST_COLS = CHUNK // 16
+PSUM_BANKS = 8
+ENTRIES_PER_COLUMN = 16
+SCALE_ROWS = 4
 ZP_COLS = T // P
-HALF = T // 2
+SPREADS_PER_BANK = 4
+SPREAD_BANKS = ZP_COLS // SPREADS_PER_BANK
+HALF_T = T // 2
+HALF_S = S // 2
+CHUNK = 256
 PAIRS = [(z, h) for z in range(PASSES) for h in range(2)]
-PIECES = [[(HALF, T), (0, HALF)]] * 3 + [[(HALF, T), (0, HALF // 2), (HALF // 2, HALF)]]
-VECTOR_TOKENS = [0, 640, 0, 640]
+VECTOR_TOKENS = [0, 512, 256, 512]
+PIECES = [[(0, 512), (512, 1280), (1280, T)]] + [[(1280, T), (512, 1280), (0, 512)]] * 3
+STRETCHES = [(0, 2), (2, 3), (3, 4)]
 
 
 def tile_picked_zeropt_none_l_kernel(tc, xT, zp, csum, w1_words, w1_scales, offs, out):
@@ -36,10 +41,9 @@ def tile_picked_zeropt_none_l_kernel(tc, xT, zp, csum, w1_words, w1_scales, offs
         keep = ctx.enter_context(tc.tile_pool(name="keep", bufs=1))
         psum = ctx.enter_context(tc.psum_pool(name="psum", bufs=1))
 
-        offsets = keep.tile([P, S // 16], U16, name="offsets")
+        offsets = keep.tile([P, S // ENTRIES_PER_COLUMN], U16, name="offsets")
         zp_rows = keep.tile([P, ZP_COLS], F32, name="zp_rows")
         nc.sync.dma_start(zp_rows[:], zp[0, :].rearrange("(n m) -> n m", m=ZP_COLS))
-
         nc.sync.dma_start(offsets[:], offs)
 
         x_rows = xT.rearrange("(z p h e) t -> z h p e t", z=PASSES, p=P, h=2, e=2)
@@ -61,38 +65,40 @@ def tile_picked_zeropt_none_l_kernel(tc, xT, zp, csum, w1_words, w1_scales, offs
         csum_cols = keep.tile([P, BLOCKS], F32, name="csum_cols")
         with nc.allow_non_contiguous_dma(reason="one value a channel"):
             nc.sync.dma_start(csum_cols[:], csum.rearrange("(b p) o -> p (b o)", p=P))
-        for q in range(4):
+        for i in range(1, len(PAIRS)):
+            load_pair(i)
+        for q in range(P // 32):
             nc.sync.dma_start(
-                w_scales[32 * q : 32 * q + 4 * PASSES, :].bitcast(I32),
-                w1_scales[:, 4 * q : 4 * q + 4, :].bitcast(I32),
+                w_scales[32 * q : 32 * q + SCALE_ROWS * PASSES, :].bitcast(I32),
+                w1_scales[:, SCALE_ROWS * q : SCALE_ROWS * (q + 1), :].bitcast(I32),
             )
-        load_pair(1)
-        load_pair(2)
-        load_pair(3)
-        w_words = keep.tile([P, PASSES, N], U32, name="w_words", align_bytes=64)
-        nc.sync.dma_start(
-            w_words[:].bitcast(I32),
-            w1_words.rearrange("z p n t -> p z (n t)").bitcast(I32),
-        )
+        w_words = []
+        for z in range(PASSES):
+            words = keep.tile([P, N], U32, name=f"w_words_{z}", align_bytes=64)
+            nc.sync.dma_start(words[:].bitcast(I32), w1_words[z].rearrange("p n t -> p (n t)").bitcast(I32))
+            w_words.append(words)
 
         neg_csum = keep.tile([P, BLOCKS], F32, name="neg_csum")
         nc.gpsimd.tensor_scalar(neg_csum[:], csum_cols[:], -1.0, 0.0, MULT, ADD)
 
         zp_window = keep.tile([P, T], F32, name="zp_window", tag="zp_window_then_picked0")
         zp_view = zp_window[:].rearrange("p (n m) -> p n m", m=ZP_COLS)
-        for q in range(ZP_COLS // 4):
-            spread = psum.tile([P, 4, P], F32, name=f"spread_{q}", tag=f"bank_{q}")
-            for i in range(4):
-                m = 4 * q + i
-                nc.tensor.transpose(spread[:, i, :], zp_rows[:, m : m + 1].to_broadcast([P, P]), ident[:])
-            nc.vector.tensor_copy(zp_view[:, :, 4 * q : 4 * q + 4], spread[:].rearrange("p i n -> p n i"))
+        for bank in range(SPREAD_BANKS):
+            spread = psum.tile([P, SPREADS_PER_BANK, P], F32, name=f"spread_{bank}", tag=f"bank_{bank}")
+            first_m = SPREADS_PER_BANK * bank
+            for i in range(SPREADS_PER_BANK):
+                column = zp_rows[:, first_m + i : first_m + i + 1]
+                nc.tensor.transpose(spread[:, i, :], column.to_broadcast([P, P]), ident[:])
+            nc.vector.tensor_copy(
+                zp_view[:, :, first_m : first_m + SPREADS_PER_BANK], spread[:].rearrange("p i n -> p n i")
+            )
         zp_picked = keep.tile([P, S], F32, name="zp_picked")
         nc.vector.tensor_copy(zp_picked[:], zp_window[:].indirect(offsets[:]))
 
         starts = [i * T - sum(VECTOR_TOKENS[: i + 1]) for i in range(len(PAIRS))]
         pairs = keep.tile([P, 2 * (starts[-1] + T)], BF16, name="pairs")
 
-        def cast(i):
+        def round_pair(i):
             for lo, hi in PIECES[i]:
                 cut = min(max(VECTOR_TOKENS[i], lo), hi)
                 for copy, a, b in ((nc.scalar.copy, cut, hi), (nc.vector.tensor_copy, lo, cut)):
@@ -105,80 +111,78 @@ def tile_picked_zeropt_none_l_kernel(tc, xT, zp, csum, w1_words, w1_scales, offs
         def window(i):
             return pairs[:, 2 * starts[i] : 2 * (starts[i] + T)].bitcast(U32)
 
-        sums = {}
-        for c in range(CHUNKS):
-            for b in range(BLOCKS):
-                sums[c, b] = psum.tile([P, CHUNK], F32, name=f"sums_{c}_{b}", tag=f"bank_{(4 + BLOCKS * c + b) % 8}")
+        def entries(lo, hi):
+            return offsets[:, lo // ENTRIES_PER_COLUMN : hi // ENTRIES_PER_COLUMN]
 
-        def multiply(z, c, codes, scales):
+        sums = {}
+        for r, (first, last) in enumerate(STRETCHES):
             for b in range(BLOCKS):
-                cols = slice(b * P, (b + 1) * P)
+                bank = (SPREAD_BANKS + BLOCKS * r + b) % PSUM_BANKS
+                sums[r, b] = psum.tile([P, (last - first) * CHUNK], F32, name=f"sums_{r}_{b}", tag=f"bank_{bank}")
+
+        def multiply(z, r, codes, scales):
+            for b in range(BLOCKS):
+                channels = slice(b * P, (b + 1) * P)
                 nc.tensor.matmul_mx(
-                    out=sums[c, b][:],
-                    lhsT=w_words[:, z, cols].bitcast(FP8X4),
-                    lhsT_scale=w_scales[4 * z : P, cols],
+                    out=sums[r, b][:],
+                    lhsT=w_words[z][:, channels].bitcast(FP8X4),
+                    lhsT_scale=w_scales[SCALE_ROWS * z : P, channels],
                     rhs=codes.bitcast(FP8X4),
                     rhs_scale=scales,
                     start=(z == 0),
                     stop=(z == PASSES - 1),
                 )
 
-        picked0 = keep.tile([P, 2, S], U32, name="picked0", tag="zp_window_then_picked0")
-        for h in range(2):
-            cast(h)
-            nc.vector.tensor_copy(picked0[:, h, :], window(h).indirect(offsets[:]))
-        woven0 = keep.tile([P, S, 2], I32, name="woven0", align_bytes=64)
-        nc.vector.tensor_copy(woven0[:], picked0[:].bitcast(I32).rearrange("p h s -> p s h"))
+        picked0 = keep.tile([P, 2 * S], U32, name="picked0", tag="zp_window_then_picked0")
+        picked0_view = picked0[:].rearrange("p (u h s) -> p u h s", h=2, s=HALF_S)
+        round_pair(0)
+        nc.vector.tensor_copy(picked0_view[:, :, 0, :], window(0).indirect(offsets[:]))
+        round_pair(1)
+        for u in range(2):
+            nc.vector.tensor_copy(picked0_view[:, u, 1, :], window(1).indirect(entries(u * HALF_S, (u + 1) * HALF_S)))
+        woven0 = [keep.tile([P, HALF_S, 2], I32, name=f"woven0_{u}", align_bytes=64) for u in range(2)]
         codes0 = keep.tile([P, S], U32, name="codes0", align_bytes=64)
         scales0 = keep.tile([P, S], U8, name="scales0", align_bytes=64)
-        nc.vector.quantize_mx(
-            out=codes0[:].bitcast(FP8X4), scales=scales0[:], in_=woven0[:].rearrange("p s h -> p (s h)").bitcast(BF16)
-        )
+        for u in range(2):
+            nc.vector.tensor_copy(woven0[u][:], picked0_view[:, u, :, :].bitcast(I32).rearrange("p h s -> p s h"))
 
-        picked1 = [keep.tile([P, 2, CHUNK], U32, name=f"picked1_{c}") for c in range(CHUNKS)]
-
-        def gather1(h, c):
-            nc.vector.tensor_copy(
-                picked1[c][:, h, :], window(2 + h).indirect(offsets[:, c * LIST_COLS : (c + 1) * LIST_COLS])
-            )
-
-        cast(2)
-        for c in range(CHUNKS):
-            gather1(0, c)
-        cast(3)
-
-        for c in range(CHUNKS):
-            multiply(0, c, codes0[:, c * CHUNK : (c + 1) * CHUNK], scales0[:, c * CHUNK : (c + 1) * CHUNK])
-
-        woven1 = [keep.tile([P, CHUNK, 2], U32, name=f"woven1_{c}", align_bytes=64) for c in range(CHUNKS)]
-        codes1 = [keep.tile([P, CHUNK], U32, name=f"codes1_{c}", align_bytes=64) for c in range(CHUNKS)]
-        scales1 = [keep.tile([P, CHUNK], U8, name=f"scales1_{c}", align_bytes=64) for c in range(CHUNKS)]
-
-        def pick(c):
-            gather1(1, c)
-            nc.scalar.copy(woven1[c][:], picked1[c][:].rearrange("p h s -> p s h"))
-
-        def quantise(c):
+        def quantize_half(u):
             nc.vector.quantize_mx(
-                out=codes1[c][:].bitcast(FP8X4),
-                scales=scales1[c][:],
-                in_=woven1[c][:].rearrange("p s h -> p (s h)").bitcast(BF16),
+                out=codes0[:, u * HALF_S : (u + 1) * HALF_S].bitcast(FP8X4),
+                scales=scales0[:, u * HALF_S : (u + 1) * HALF_S],
+                in_=woven0[u][:].rearrange("p s h -> p (s h)").bitcast(BF16),
             )
-            multiply(1, c, codes1[c][:], scales1[c][:])
 
-        def finish(c):
-            cols = slice(c * CHUNK, (c + 1) * CHUNK)
+        picked1 = keep.tile([P, 2 * S], U32, name="picked1")
+        picked1_view = picked1[:].rearrange("p (c h s) -> p c h s", h=2, s=CHUNK)
+        round_pair(2)
+        quantize_half(0)
+        nc.vector.tensor_copy(picked1_view[:, :, 0, :], window(2).indirect(offsets[:]))
+        quantize_half(1)
+        round_pair(3)
+
+        for r, (first, last) in enumerate(STRETCHES):
+            multiply(0, r, codes0[:, first * CHUNK : last * CHUNK], scales0[:, first * CHUNK : last * CHUNK])
+
+        for r, (first, last) in enumerate(STRETCHES):
+            width = (last - first) * CHUNK
+            woven1 = keep.tile([P, 2 * width], U32, name=f"woven1_{r}", align_bytes=64)
+            codes1 = keep.tile([P, width], U32, name=f"codes1_{r}", align_bytes=64)
+            scales1 = keep.tile([P, width], U8, name=f"scales1_{r}", align_bytes=64)
+            for c in range(first, last):
+                nc.vector.tensor_copy(picked1_view[:, c, 1, :], window(3).indirect(entries(c * CHUNK, (c + 1) * CHUNK)))
+                nc.scalar.copy(
+                    woven1[:, 2 * (c - first) * CHUNK : 2 * (c - first + 1) * CHUNK].rearrange("p (s h) -> p s h", h=2),
+                    picked1_view[:, c, :, :].rearrange("p h s -> p s h"),
+                )
+            nc.vector.quantize_mx(out=codes1[:].bitcast(FP8X4), scales=scales1[:], in_=woven1[:].bitcast(BF16))
+            multiply(1, r, codes1[:], scales1[:])
+
+        for r, (first, last) in enumerate(STRETCHES):
+            cols = slice(first * CHUNK, last * CHUNK)
             for b in range(BLOCKS):
-                result = keep.tile([P, CHUNK], F32, name=f"result_{c}_{b}")
+                result = keep.tile([P, (last - first) * CHUNK], F32, name=f"result_{r}_{b}")
                 nc.vector.scalar_tensor_tensor(
-                    result[:], zp_picked[:, cols], neg_csum[:, b : b + 1], sums[c, b][:], MULT, ADD
+                    result[:], zp_picked[:, cols], neg_csum[:, b : b + 1], sums[r, b][:], MULT, ADD
                 )
                 nc.sync.dma_start(out[b * P : (b + 1) * P, cols], result[:])
-
-        for step in range(CHUNKS + 2):
-            if step < CHUNKS:
-                pick(step)
-            if 1 <= step <= CHUNKS:
-                quantise(step - 1)
-            if step >= 2:
-                finish(step - 2)

@@ -30,8 +30,8 @@ HALF_T = T // 2
 HALF_S = S // 2
 CHUNK = 256
 PAIRS = [(z, h) for z in range(PASSES) for h in range(2)]
-VECTOR_TOKENS = [0, 512, 256, 512]
-PIECES = [[(0, 512), (512, 1280), (1280, T)]] + [[(1280, T), (512, 1280), (0, 512)]] * 3
+VECTOR_TOKENS = [0, 640, 256, 384]
+PIECES = [[(HALF_T, T), (0, HALF_T)]] * 3 + [[(1280, T), (512, 1280), (0, 512)]]
 STRETCHES = [(0, 2), (2, 3), (3, 4)]
 
 
@@ -60,26 +60,23 @@ def tile_picked_zeropt_none_l_kernel(tc, xT, zp, csum, w1_words, w1_scales, offs
         nc.gpsimd.memset(w_scales[:].bitcast(I32), 0)
         ident = keep.tile([P, P], F32, name="ident")
         make_identity(nc, ident[:])
+        csum_rows = keep.tile([P, P], F32, name="csum_rows")
+        nc.gpsimd.memset(csum_rows[:], 0.0)
 
         load_pair(0)
-        csum_cols = keep.tile([P, BLOCKS], F32, name="csum_cols")
-        with nc.allow_non_contiguous_dma(reason="one value a channel"):
-            nc.sync.dma_start(csum_cols[:], csum.rearrange("(b p) o -> p (b o)", p=P))
-        for i in range(1, len(PAIRS)):
-            load_pair(i)
+        nc.sync.dma_start(csum_rows[0:BLOCKS, :], csum.rearrange("(b p) o -> b (p o)", p=P))
         for q in range(P // 32):
             nc.sync.dma_start(
                 w_scales[32 * q : 32 * q + SCALE_ROWS * PASSES, :].bitcast(I32),
                 w1_scales[:, SCALE_ROWS * q : SCALE_ROWS * (q + 1), :].bitcast(I32),
             )
-        w_words = []
-        for z in range(PASSES):
-            words = keep.tile([P, N], U32, name=f"w_words_{z}", align_bytes=64)
-            nc.sync.dma_start(words[:].bitcast(I32), w1_words[z].rearrange("p n t -> p (n t)").bitcast(I32))
-            w_words.append(words)
-
-        neg_csum = keep.tile([P, BLOCKS], F32, name="neg_csum")
-        nc.gpsimd.tensor_scalar(neg_csum[:], csum_cols[:], -1.0, 0.0, MULT, ADD)
+        for i in range(1, len(PAIRS)):
+            load_pair(i)
+        w_words = keep.tile([P, PASSES, N], U32, name="w_words", align_bytes=64)
+        nc.sync.dma_start(
+            w_words[:].bitcast(I32),
+            w1_words.rearrange("z p n t -> p z (n t)").bitcast(I32),
+        )
 
         zp_window = keep.tile([P, T], F32, name="zp_window", tag="zp_window_then_picked0")
         zp_view = zp_window[:].rearrange("p (n m) -> p n m", m=ZP_COLS)
@@ -95,8 +92,7 @@ def tile_picked_zeropt_none_l_kernel(tc, xT, zp, csum, w1_words, w1_scales, offs
         zp_picked = keep.tile([P, S], F32, name="zp_picked")
         nc.vector.tensor_copy(zp_picked[:], zp_window[:].indirect(offsets[:]))
 
-        starts = [i * T - sum(VECTOR_TOKENS[: i + 1]) for i in range(len(PAIRS))]
-        pairs = keep.tile([P, 2 * (starts[-1] + T)], BF16, name="pairs")
+        pairs = keep.tile([P, 2 * len(PAIRS) * T], BF16, name="pairs")
 
         def round_pair(i):
             for lo, hi in PIECES[i]:
@@ -104,12 +100,12 @@ def tile_picked_zeropt_none_l_kernel(tc, xT, zp, csum, w1_words, w1_scales, offs
                 for copy, a, b in ((nc.scalar.copy, cut, hi), (nc.vector.tensor_copy, lo, cut)):
                     if a < b:
                         copy(
-                            pairs[:, 2 * (starts[i] + a) : 2 * (starts[i] + b)].rearrange("p (c e) -> p c e", e=2),
+                            pairs[:, 2 * (i * T + a) : 2 * (i * T + b)].rearrange("p (c e) -> p c e", e=2),
                             raw[i, lo][:, :, a - lo : b - lo].rearrange("p e c -> p c e"),
                         )
 
         def window(i):
-            return pairs[:, 2 * starts[i] : 2 * (starts[i] + T)].bitcast(U32)
+            return pairs[:, 2 * i * T : 2 * (i + 1) * T].bitcast(U32)
 
         def entries(lo, hi):
             return offsets[:, lo // ENTRIES_PER_COLUMN : hi // ENTRIES_PER_COLUMN]
@@ -125,7 +121,7 @@ def tile_picked_zeropt_none_l_kernel(tc, xT, zp, csum, w1_words, w1_scales, offs
                 channels = slice(b * P, (b + 1) * P)
                 nc.tensor.matmul_mx(
                     out=sums[r, b][:],
-                    lhsT=w_words[z][:, channels].bitcast(FP8X4),
+                    lhsT=w_words[:, z, channels].bitcast(FP8X4),
                     lhsT_scale=w_scales[SCALE_ROWS * z : P, channels],
                     rhs=codes.bitcast(FP8X4),
                     rhs_scale=scales,
@@ -145,8 +141,7 @@ def tile_picked_zeropt_none_l_kernel(tc, xT, zp, csum, w1_words, w1_scales, offs
         scales0 = keep.tile([P, S], U8, name="scales0", align_bytes=64)
         for u in range(2):
             nc.vector.tensor_copy(woven0[u][:], picked0_view[:, u, :, :].bitcast(I32).rearrange("p h s -> p s h"))
-
-        def quantize_half(u):
+        for u in range(2):
             nc.vector.quantize_mx(
                 out=codes0[:, u * HALF_S : (u + 1) * HALF_S].bitcast(FP8X4),
                 scales=scales0[:, u * HALF_S : (u + 1) * HALF_S],
@@ -156,9 +151,7 @@ def tile_picked_zeropt_none_l_kernel(tc, xT, zp, csum, w1_words, w1_scales, offs
         picked1 = keep.tile([P, 2 * S], U32, name="picked1")
         picked1_view = picked1[:].rearrange("p (c h s) -> p c h s", h=2, s=CHUNK)
         round_pair(2)
-        quantize_half(0)
         nc.vector.tensor_copy(picked1_view[:, :, 0, :], window(2).indirect(offsets[:]))
-        quantize_half(1)
         round_pair(3)
 
         for r, (first, last) in enumerate(STRETCHES):
@@ -177,6 +170,11 @@ def tile_picked_zeropt_none_l_kernel(tc, xT, zp, csum, w1_words, w1_scales, offs
                 )
             nc.vector.quantize_mx(out=codes1[:].bitcast(FP8X4), scales=scales1[:], in_=woven1[:].bitcast(BF16))
             multiply(1, r, codes1[:], scales1[:])
+
+        csum_cols = psum.tile([P, P], F32, name="csum_cols", tag="bank_2")
+        nc.tensor.transpose(csum_cols[:], csum_rows[:], ident[:])
+        neg_csum = keep.tile([P, BLOCKS], F32, name="neg_csum")
+        nc.scalar.activation(neg_csum[:], csum_cols[:, 0:BLOCKS], mybir.ActivationFunctionType.Copy, scale=-1.0)
 
         for r, (first, last) in enumerate(STRETCHES):
             cols = slice(first * CHUNK, last * CHUNK)

@@ -30,7 +30,8 @@ HALF_T = T // 2
 HALF_S = S // 2
 CHUNK = 256
 PAIRS = [(z, h) for z in range(PASSES) for h in range(2)]
-VECTOR_TOKENS = [0, 640, 256, 384]
+VECTOR_TOKENS = [0, 640, 256, 352]
+GPSIMD_TOKENS = {(0, 0): 448, (3, 512): 256}
 PIECES = [[(HALF_T, T), (0, HALF_T)]] * 3 + [[(1280, T), (512, 1280), (0, 512)]]
 STRETCHES = [(0, 2), (2, 3), (3, 4)]
 
@@ -94,10 +95,14 @@ def tile_picked_zeropt_none_l_kernel(tc, xT, zp, csum, w1_words, w1_scales, offs
 
         pairs = keep.tile([P, 2 * len(PAIRS) * T], BF16, name="pairs")
 
+        def gpsimd_round(rounded, values):
+            nc.gpsimd.tensor_scalar(rounded, values, 1.0, 0.0, MULT, ADD)
+
         def round_pair(i):
             for lo, hi in PIECES[i]:
                 cut = min(max(VECTOR_TOKENS[i], lo), hi)
-                for copy, a, b in ((nc.scalar.copy, cut, hi), (nc.vector.tensor_copy, lo, cut)):
+                side = cut + GPSIMD_TOKENS.get((i, lo), 0)
+                for copy, a, b in ((nc.scalar.copy, side, hi), (gpsimd_round, cut, side), (nc.vector.tensor_copy, lo, cut)):
                     if a < b:
                         copy(
                             pairs[:, 2 * (i * T + a) : 2 * (i * T + b)].rearrange("p (c e) -> p c e", e=2),

@@ -66,11 +66,6 @@ def tile_picked_zeropt_none_l_kernel(tc, xT, zp, csum, w1_words, w1_scales, offs
 
         load_pair(0)
         nc.sync.dma_start(csum_rows[0:BLOCKS, :], csum.rearrange("(b p) o -> b (p o)", p=P))
-        for q in range(P // 32):
-            nc.sync.dma_start(
-                w_scales[32 * q : 32 * q + SCALE_ROWS * PASSES, :].bitcast(I32),
-                w1_scales[:, SCALE_ROWS * q : SCALE_ROWS * (q + 1), :].bitcast(I32),
-            )
         for i in range(1, len(PAIRS)):
             load_pair(i)
         w_words = keep.tile([P, PASSES, N], U32, name="w_words", align_bytes=64)
@@ -78,6 +73,12 @@ def tile_picked_zeropt_none_l_kernel(tc, xT, zp, csum, w1_words, w1_scales, offs
             w_words[:].bitcast(I32),
             w1_words.rearrange("z p n t -> p z (n t)").bitcast(I32),
         )
+
+        for q in range(P // 32):
+            nc.sync.dma_start(
+                w_scales[32 * q : 32 * q + SCALE_ROWS * PASSES, :].bitcast(I32),
+                w1_scales[:, SCALE_ROWS * q : SCALE_ROWS * (q + 1), :].bitcast(I32),
+            )
 
         zp_window = keep.tile([P, T], F32, name="zp_window", tag="zp_window_then_picked0")
         zp_view = zp_window[:].rearrange("p (n m) -> p n m", m=ZP_COLS)

@@ -45,7 +45,6 @@ def tile_picked_zeropt_none_l_kernel(tc, xT, zp, csum, w1_words, w1_scales, offs
         offsets = keep.tile([P, S // ENTRIES_PER_COLUMN], U16, name="offsets")
         zp_rows = keep.tile([P, ZP_COLS], F32, name="zp_rows")
         nc.sync.dma_start(zp_rows[:], zp[0, :].rearrange("(n m) -> n m", m=ZP_COLS))
-        nc.sync.dma_start(offsets[:], offs)
 
         x_rows = xT.rearrange("(z p h e) t -> z h p e t", z=PASSES, p=P, h=2, e=2)
         raw = {}
@@ -56,6 +55,8 @@ def tile_picked_zeropt_none_l_kernel(tc, xT, zp, csum, w1_words, w1_scales, offs
                 piece = keep.tile([P, 2, hi - lo], F32, name=f"raw_{i}_{lo}")
                 nc.sync.dma_start(piece[:], x_rows[z, h, :, :, lo:hi])
                 raw[i, lo] = piece
+                if (i, lo) == (0, HALF_T):
+                    nc.sync.dma_start(offsets[:], offs)
 
         w_scales = keep.tile([P, N], U8, name="w_scales", align_bytes=64)
         nc.gpsimd.memset(w_scales[:].bitcast(I32), 0)
@@ -183,10 +184,15 @@ def tile_picked_zeropt_none_l_kernel(tc, xT, zp, csum, w1_words, w1_scales, offs
         nc.scalar.activation(neg_csum[:], csum_cols[:, 0:BLOCKS], mybir.ActivationFunctionType.Copy, scale=-1.0)
 
         for r, (first, last) in enumerate(STRETCHES):
-            cols = slice(first * CHUNK, last * CHUNK)
             for b in range(BLOCKS):
                 result = keep.tile([P, (last - first) * CHUNK], F32, name=f"result_{r}_{b}")
-                nc.vector.scalar_tensor_tensor(
-                    result[:], zp_picked[:, cols], neg_csum[:, b : b + 1], sums[r, b][:], MULT, ADD
-                )
-                nc.sync.dma_start(out[b * P : (b + 1) * P, cols], result[:])
+                width = (last - first) * CHUNK
+                step = CHUNK if (r, b) == (0, 0) else width
+                for lo in range(0, width, step):
+                    part = slice(lo, lo + step)
+                    columns = slice(first * CHUNK + lo, first * CHUNK + lo + step)
+                    nc.vector.scalar_tensor_tensor(
+                        result[:, part], zp_picked[:, columns], neg_csum[:, b : b + 1], sums[r, b][:, part], MULT, ADD
+                    )
+                    queue = nc.sync if b == 0 else nc.scalar
+                    queue.dma_start(out[b * P : (b + 1) * P, columns], result[:, part])

@@ -30,9 +30,14 @@ HALF_T = T // 2
 HALF_S = S // 2
 CHUNK = 256
 PAIRS = [(z, h) for z in range(PASSES) for h in range(2)]
-VECTOR_TOKENS = [0, 640, 256, 352]
-GPSIMD_TOKENS = {(0, 0): 448, (3, 512): 256}
-PIECES = [[(HALF_T, T), (0, HALF_T)]] * 3 + [[(1280, T), (512, 1280), (0, 512)]]
+VECTOR_TOKENS = [0, 512, 448, 256]
+GPSIMD_TOKENS = {(0, 0): 448, (1, 768): 512, (2, HALF_T): 448, (3, HALF_T): 512, (3, 256): 288}
+PIECES = [
+    [(HALF_T, T), (0, HALF_T)],
+    [(768, T), (0, 768)],
+    [(HALF_T, T), (0, HALF_T)],
+    [(HALF_T, T), (256, HALF_T), (0, 256)],
+]
 STRETCHES = [(0, 2), (2, 3), (3, 4)]
 
 
@@ -48,12 +53,16 @@ def tile_picked_zeropt_none_l_kernel(tc, xT, zp, csum, w1_words, w1_scales, offs
 
         x_rows = xT.rearrange("(z p h e) t -> z h p e t", z=PASSES, p=P, h=2, e=2)
         raw = {}
+        pairs = keep.tile([P, 2 * (len(PAIRS) * T + HALF_T)], BF16, name="pairs")
 
         def load_pair(i):
             z, h = PAIRS[i]
             for lo, hi in PIECES[i]:
-                piece = keep.tile([P, 2, hi - lo], F32, name=f"raw_{i}_{lo}")
-                nc.sync.dma_start(piece[:], x_rows[z, h, :, :, lo:hi])
+                if (i, lo) == (2, 0):
+                    piece = pairs[:, 2 * (3 * T + HALF_T) :].bitcast(F32).rearrange("p (e c) -> p e c", e=2)
+                else:
+                    piece = keep.tile([P, 2, hi - lo], F32, name=f"raw_{i}_{lo}")[:]
+                nc.sync.dma_start(piece, x_rows[z, h, :, :, lo:hi])
                 raw[i, lo] = piece
                 if (i, lo) == (0, HALF_T):
                     nc.sync.dma_start(offsets[:], offs)
@@ -95,7 +104,6 @@ def tile_picked_zeropt_none_l_kernel(tc, xT, zp, csum, w1_words, w1_scales, offs
         zp_picked = keep.tile([P, S], F32, name="zp_picked")
         nc.vector.tensor_copy(zp_picked[:], zp_window[:].indirect(offsets[:]))
 
-        pairs = keep.tile([P, 2 * len(PAIRS) * T], BF16, name="pairs")
 
         def gpsimd_round(rounded, values):
             nc.gpsimd.tensor_scalar(rounded, values, 1.0, 0.0, MULT, ADD)
@@ -146,18 +154,22 @@ def tile_picked_zeropt_none_l_kernel(tc, xT, zp, csum, w1_words, w1_scales, offs
         woven0 = [keep.tile([P, HALF_S, 2], I32, name=f"woven0_{u}", align_bytes=64) for u in range(2)]
         codes0 = keep.tile([P, S], U32, name="codes0", align_bytes=64)
         scales0 = keep.tile([P, S], U8, name="scales0", align_bytes=64)
-        for u in range(2):
-            nc.vector.tensor_copy(woven0[u][:], picked0_view[:, u, :, :].bitcast(I32).rearrange("p h s -> p s h"))
-        for u in range(2):
+        nc.scalar.copy(woven0[0][:].bitcast(U32), picked0_view[:, 0, :, :].rearrange("p h s -> p s h"))
+        nc.vector.tensor_copy(woven0[1][:], picked0_view[:, 1, :, :].bitcast(I32).rearrange("p h s -> p s h"))
+
+        def quantise0(u):
             nc.vector.quantize_mx(
                 out=codes0[:, u * HALF_S : (u + 1) * HALF_S].bitcast(FP8X4),
                 scales=scales0[:, u * HALF_S : (u + 1) * HALF_S],
                 in_=woven0[u][:].rearrange("p s h -> p (s h)").bitcast(BF16),
             )
 
+        quantise0(1)
+
         picked1 = keep.tile([P, 2 * S], U32, name="picked1")
         picked1_view = picked1[:].rearrange("p (c h s) -> p c h s", h=2, s=CHUNK)
         round_pair(2)
+        quantise0(0)
         nc.vector.tensor_copy(picked1_view[:, :, 0, :], window(2).indirect(offsets[:]))
         round_pair(3)
 

@@ -16,11 +16,11 @@ U8 = mybir.dt.uint8
 FP8X4 = mybir.dt.float8_e4m3fn_x4
 MULT = mybir.AluOpType.mult
 ADD = mybir.AluOpType.add
+COPY = mybir.ActivationFunctionType.Copy
 
 P = 128
 PASSES = K // (4 * P)
 BLOCKS = N // P
-PSUM_BANKS = 8
 ENTRIES_PER_COLUMN = 16
 SCALE_ROWS = 4
 ZP_COLS = T // P
@@ -29,16 +29,17 @@ SPREAD_BANKS = ZP_COLS // SPREADS_PER_BANK
 HALF_T = T // 2
 HALF_S = S // 2
 CHUNK = 256
-PAIRS = [(z, h) for z in range(PASSES) for h in range(2)]
-VECTOR_TOKENS = [0, 512, 448, 256]
-GPSIMD_TOKENS = {(0, 0): 448, (1, 768): 512, (2, HALF_T): 448, (3, HALF_T): 512, (3, 256): 288}
+CHUNKS = S // CHUNK
+PAIRS = [(0, 0), (0, 1), (1, 0)]
+VECTOR_TOKENS = [0, 512, 448]
+GPSIMD_TOKENS = {(0, 0): 448, (1, 768): 512, (2, HALF_T): 448}
 PIECES = [
     [(HALF_T, T), (0, HALF_T)],
     [(768, T), (0, 768)],
     [(HALF_T, T), (0, HALF_T)],
-    [(HALF_T, T), (256, HALF_T), (0, 256)],
 ]
-STRETCHES = [(0, 2), (2, 3), (3, 4)]
+PLANE_PIECES = {2: [(0, HALF_T), (HALF_T, T)], 3: [(0, 768), (768, 1536), (1536, T)]}
+SCALAR_RUNS = [(256, 640), (640, 1024)]
 
 
 def tile_picked_zeropt_none_l_kernel(tc, xT, zp, csum, w1_words, w1_scales, offs, out):
@@ -53,19 +54,21 @@ def tile_picked_zeropt_none_l_kernel(tc, xT, zp, csum, w1_words, w1_scales, offs
 
         x_rows = xT.rearrange("(z p h e) t -> z h p e t", z=PASSES, p=P, h=2, e=2)
         raw = {}
-        pairs = keep.tile([P, 2 * (len(PAIRS) * T + HALF_T)], BF16, name="pairs")
 
         def load_pair(i):
             z, h = PAIRS[i]
             for lo, hi in PIECES[i]:
-                if (i, lo) == (2, 0):
-                    piece = pairs[:, 2 * (3 * T + HALF_T) :].bitcast(F32).rearrange("p (e c) -> p e c", e=2)
-                else:
-                    piece = keep.tile([P, 2, hi - lo], F32, name=f"raw_{i}_{lo}")[:]
+                piece = keep.tile([P, 2, hi - lo], F32, name=f"raw_{i}_{lo}")[:]
                 nc.sync.dma_start(piece, x_rows[z, h, :, :, lo:hi])
                 raw[i, lo] = piece
                 if (i, lo) == (0, HALF_T):
                     nc.sync.dma_start(offsets[:], offs)
+
+        planes = {t: keep.tile([P, T], F32, name=f"plane_{t}") for t in (2, 3)}
+
+        def load_plane(t):
+            for lo, hi in PLANE_PIECES[t]:
+                nc.sync.dma_start(planes[t][:, lo:hi], x_rows[1, 1, :, t - 2, lo:hi])
 
         w_scales = keep.tile([P, N], U8, name="w_scales", align_bytes=64)
         nc.gpsimd.memset(w_scales[:].bitcast(I32), 0)
@@ -73,22 +76,24 @@ def tile_picked_zeropt_none_l_kernel(tc, xT, zp, csum, w1_words, w1_scales, offs
         make_identity(nc, ident[:])
         csum_rows = keep.tile([P, P], F32, name="csum_rows")
         nc.gpsimd.memset(csum_rows[:], 0.0)
+        w_words = [keep.tile([P, N], U32, name=f"w_words_{z}", align_bytes=64) for z in range(PASSES)]
+
+        def load_words(z):
+            nc.sync.dma_start(w_words[z][:].bitcast(I32), w1_words[z].rearrange("p n t -> p (n t)").bitcast(I32))
 
         load_pair(0)
         nc.sync.dma_start(csum_rows[0:BLOCKS, :], csum.rearrange("(b p) o -> b (p o)", p=P))
-        for i in range(1, len(PAIRS)):
-            load_pair(i)
-        w_words = keep.tile([P, PASSES, N], U32, name="w_words", align_bytes=64)
-        nc.sync.dma_start(
-            w_words[:].bitcast(I32),
-            w1_words.rearrange("z p n t -> p z (n t)").bitcast(I32),
-        )
-
+        load_pair(1)
         for q in range(P // 32):
             nc.sync.dma_start(
                 w_scales[32 * q : 32 * q + SCALE_ROWS * PASSES, :].bitcast(I32),
                 w1_scales[:, SCALE_ROWS * q : SCALE_ROWS * (q + 1), :].bitcast(I32),
             )
+        load_pair(2)
+        load_plane(2)
+        load_words(0)
+        load_plane(3)
+        load_words(1)
 
         zp_window = keep.tile([P, T], F32, name="zp_window", tag="zp_window_then_picked0")
         zp_view = zp_window[:].rearrange("p (n m) -> p n m", m=ZP_COLS)
@@ -104,6 +109,7 @@ def tile_picked_zeropt_none_l_kernel(tc, xT, zp, csum, w1_words, w1_scales, offs
         zp_picked = keep.tile([P, S], F32, name="zp_picked")
         nc.vector.tensor_copy(zp_picked[:], zp_window[:].indirect(offsets[:]))
 
+        pairs = [keep.tile([P, 2 * T], BF16, name=f"pair_{i}") for i in range(len(PAIRS))]
 
         def gpsimd_round(rounded, values):
             nc.gpsimd.tensor_scalar(rounded, values, 1.0, 0.0, MULT, ADD)
@@ -115,39 +121,26 @@ def tile_picked_zeropt_none_l_kernel(tc, xT, zp, csum, w1_words, w1_scales, offs
                 for copy, a, b in ((nc.scalar.copy, side, hi), (gpsimd_round, cut, side), (nc.vector.tensor_copy, lo, cut)):
                     if a < b:
                         copy(
-                            pairs[:, 2 * (i * T + a) : 2 * (i * T + b)].rearrange("p (c e) -> p c e", e=2),
+                            pairs[i][:, 2 * a : 2 * b].rearrange("p (c e) -> p c e", e=2),
                             raw[i, lo][:, :, a - lo : b - lo].rearrange("p e c -> p c e"),
                         )
 
         def window(i):
-            return pairs[:, 2 * i * T : 2 * (i + 1) * T].bitcast(U32)
+            return pairs[i][:].bitcast(U32)
 
         def entries(lo, hi):
             return offsets[:, lo // ENTRIES_PER_COLUMN : hi // ENTRIES_PER_COLUMN]
-
-        sums = {}
-        for r, (first, last) in enumerate(STRETCHES):
-            for b in range(BLOCKS):
-                bank = (SPREAD_BANKS + BLOCKS * r + b) % PSUM_BANKS
-                sums[r, b] = psum.tile([P, (last - first) * CHUNK], F32, name=f"sums_{r}_{b}", tag=f"bank_{bank}")
-
-        def multiply(z, r, codes, scales):
-            for b in range(BLOCKS):
-                channels = slice(b * P, (b + 1) * P)
-                nc.tensor.matmul_mx(
-                    out=sums[r, b][:],
-                    lhsT=w_words[:, z, channels].bitcast(FP8X4),
-                    lhsT_scale=w_scales[SCALE_ROWS * z : P, channels],
-                    rhs=codes.bitcast(FP8X4),
-                    rhs_scale=scales,
-                    start=(z == 0),
-                    stop=(z == PASSES - 1),
-                )
 
         picked0 = keep.tile([P, 2 * S], U32, name="picked0", tag="zp_window_then_picked0")
         picked0_view = picked0[:].rearrange("p (u h s) -> p u h s", h=2, s=HALF_S)
         round_pair(0)
         nc.vector.tensor_copy(picked0_view[:, :, 0, :], window(0).indirect(offsets[:]))
+
+        csum_cols = psum.tile([P, P], F32, name="csum_cols", tag="bank_4")
+        nc.tensor.transpose(csum_cols[:], csum_rows[:], ident[:])
+        neg_csum = keep.tile([P, BLOCKS], F32, name="neg_csum")
+        nc.scalar.activation(neg_csum[:], csum_cols[:, 0:BLOCKS], COPY, scale=-1.0)
+
         round_pair(1)
         for u in range(2):
             nc.vector.tensor_copy(picked0_view[:, u, 1, :], window(1).indirect(entries(u * HALF_S, (u + 1) * HALF_S)))
@@ -165,46 +158,71 @@ def tile_picked_zeropt_none_l_kernel(tc, xT, zp, csum, w1_words, w1_scales, offs
             )
 
         quantise0(1)
-
-        picked1 = keep.tile([P, 2 * S], U32, name="picked1")
-        picked1_view = picked1[:].rearrange("p (c h s) -> p c h s", h=2, s=CHUNK)
         round_pair(2)
         quantise0(0)
-        nc.vector.tensor_copy(picked1_view[:, :, 0, :], window(2).indirect(offsets[:]))
-        round_pair(3)
 
-        for r, (first, last) in enumerate(STRETCHES):
-            multiply(0, r, codes0[:, first * CHUNK : last * CHUNK], scales0[:, first * CHUNK : last * CHUNK])
-
-        for r, (first, last) in enumerate(STRETCHES):
-            width = (last - first) * CHUNK
-            woven1 = keep.tile([P, 2 * width], U32, name=f"woven1_{r}", align_bytes=64)
-            codes1 = keep.tile([P, width], U32, name=f"codes1_{r}", align_bytes=64)
-            scales1 = keep.tile([P, width], U8, name=f"scales1_{r}", align_bytes=64)
-            for c in range(first, last):
-                nc.vector.tensor_copy(picked1_view[:, c, 1, :], window(3).indirect(entries(c * CHUNK, (c + 1) * CHUNK)))
-                nc.scalar.copy(
-                    woven1[:, 2 * (c - first) * CHUNK : 2 * (c - first + 1) * CHUNK].rearrange("p (s h) -> p s h", h=2),
-                    picked1_view[:, c, :, :].rearrange("p h s -> p s h"),
-                )
-            nc.vector.quantize_mx(out=codes1[:].bitcast(FP8X4), scales=scales1[:], in_=woven1[:].bitcast(BF16))
-            multiply(1, r, codes1[:], scales1[:])
-
-        csum_cols = psum.tile([P, P], F32, name="csum_cols", tag="bank_2")
-        nc.tensor.transpose(csum_cols[:], csum_rows[:], ident[:])
-        neg_csum = keep.tile([P, BLOCKS], F32, name="neg_csum")
-        nc.scalar.activation(neg_csum[:], csum_cols[:, 0:BLOCKS], mybir.ActivationFunctionType.Copy, scale=-1.0)
-
-        for r, (first, last) in enumerate(STRETCHES):
+        sums = {}
+        for c in range(CHUNKS):
             for b in range(BLOCKS):
-                result = keep.tile([P, (last - first) * CHUNK], F32, name=f"result_{r}_{b}")
-                width = (last - first) * CHUNK
-                step = CHUNK if (r, b) == (0, 0) else width
-                for lo in range(0, width, step):
-                    part = slice(lo, lo + step)
-                    columns = slice(first * CHUNK + lo, first * CHUNK + lo + step)
-                    nc.vector.scalar_tensor_tensor(
-                        result[:, part], zp_picked[:, columns], neg_csum[:, b : b + 1], sums[r, b][:, part], MULT, ADD
-                    )
-                    queue = nc.sync if b == 0 else nc.scalar
-                    queue.dma_start(out[b * P : (b + 1) * P, columns], result[:, part])
+                sums[c, b] = psum.tile([P, CHUNK], F32, name=f"sums_{c}_{b}", tag=f"bank_{BLOCKS * c + b}")
+
+        def multiply(z, c, codes, scales):
+            for b in range(BLOCKS):
+                channels = slice(b * P, (b + 1) * P)
+                nc.tensor.matmul_mx(
+                    out=sums[c, b][:],
+                    lhsT=w_words[z][:, channels].bitcast(FP8X4),
+                    lhsT_scale=w_scales[SCALE_ROWS * z : P, channels],
+                    rhs=codes.bitcast(FP8X4),
+                    rhs_scale=scales,
+                    start=(z == 0),
+                    stop=(z == PASSES - 1),
+                )
+
+        for c in range(CHUNKS):
+            multiply(0, c, codes0[:, c * CHUNK : (c + 1) * CHUNK], scales0[:, c * CHUNK : (c + 1) * CHUNK])
+
+        woven1 = keep.tile([P, 4 * S], BF16, name="woven1", align_bytes=64)
+        woven1_words = woven1[:].bitcast(U32).rearrange("p (s h) -> p s h", h=2)
+        woven1_slots = woven1[:].rearrange("p (s t) -> p s t", t=4)
+        for lo, hi in SCALAR_RUNS + [(0, CHUNK)]:
+            nc.vector.tensor_copy(woven1_words[:, lo:hi, 0], window(2).indirect(entries(lo, hi)))
+
+        rounded = {t: keep.tile([P, T], BF16, name=f"rounded_{t}") for t in (2, 3)}
+        nc.scalar.copy(rounded[2][:, 0:HALF_T], planes[2][:, 0:HALF_T])
+        nc.scalar.copy(rounded[2][:, HALF_T:1536], planes[2][:, HALF_T:1536])
+        gpsimd_round(rounded[2][:, 1536:T], planes[2][:, 1536:T])
+        for lo, hi in SCALAR_RUNS:
+            nc.scalar.activation(woven1_slots[:, lo:hi, 2], rounded[2][:].indirect(entries(lo, hi)), COPY)
+        nc.vector.tensor_copy(woven1_slots[:, 0:CHUNK, 2], planes[2][:].indirect(entries(0, CHUNK)))
+        for lo, hi in PLANE_PIECES[3]:
+            gpsimd_round(rounded[3][:, lo:hi], planes[3][:, lo:hi])
+
+        codes1 = keep.tile([P, S], U32, name="codes1", align_bytes=64)
+        scales1 = keep.tile([P, S], U8, name="scales1", align_bytes=64)
+
+        def finish(c):
+            lo, hi = c * CHUNK, (c + 1) * CHUNK
+            if c == 0:
+                nc.vector.tensor_copy(woven1_slots[:, lo:hi, 3], planes[3][:].indirect(entries(lo, hi)))
+            else:
+                nc.scalar.activation(woven1_slots[:, lo:hi, 3], rounded[3][:].indirect(entries(lo, hi)), COPY)
+            nc.vector.quantize_mx(
+                out=codes1[:, lo:hi].bitcast(FP8X4), scales=scales1[:, lo:hi], in_=woven1[:, 4 * lo : 4 * hi]
+            )
+            multiply(1, c, codes1[:, lo:hi], scales1[:, lo:hi])
+
+        def store(c):
+            columns = slice(c * CHUNK, (c + 1) * CHUNK)
+            for b in range(BLOCKS):
+                result = keep.tile([P, CHUNK], F32, name=f"result_{c}_{b}")
+                nc.vector.scalar_tensor_tensor(
+                    result[:], zp_picked[:, columns], neg_csum[:, b : b + 1], sums[c, b][:], MULT, ADD
+                )
+                nc.sync.dma_start(out[b * P : (b + 1) * P, columns], result[:])
+
+        finish(0)
+        for c in range(1, CHUNKS):
+            finish(c)
+            store(c - 1)
+        store(CHUNKS - 1)

@@ -31,15 +31,14 @@ HALF_S = S // 2
 CHUNK = 256
 CHUNKS = S // CHUNK
 PAIRS = [(0, 0), (0, 1), (1, 0)]
-VECTOR_TOKENS = [0, 512, 448]
-GPSIMD_TOKENS = {(0, 0): 448, (1, 768): 512, (2, HALF_T): 448}
+VECTOR_TOKENS = [0, 512, 256]
+GPSIMD_TOKENS = {(0, 0): 448, (1, 768): 512, (2, 1280): 768, (2, 512): 192}
 PIECES = [
     [(HALF_T, T), (0, HALF_T)],
     [(768, T), (0, 768)],
-    [(HALF_T, T), (0, HALF_T)],
+    [(1280, T), (512, 1280), (0, 512)],
 ]
 PLANE_PIECES = {2: [(0, HALF_T), (HALF_T, T)], 3: [(0, 768), (768, 1536), (1536, T)]}
-SCALAR_RUNS = [(256, 640), (640, 1024)]
 
 
 def tile_picked_zeropt_none_l_kernel(tc, xT, zp, csum, w1_words, w1_scales, offs, out):
@@ -69,6 +68,8 @@ def tile_picked_zeropt_none_l_kernel(tc, xT, zp, csum, w1_words, w1_scales, offs
         def load_plane(t):
             for lo, hi in PLANE_PIECES[t]:
                 nc.sync.dma_start(planes[t][:, lo:hi], x_rows[1, 1, :, t - 2, lo:hi])
+                if (t, lo) == (3, 0):
+                    load_words(0)
 
         w_scales = keep.tile([P, N], U8, name="w_scales", align_bytes=64)
         nc.gpsimd.memset(w_scales[:].bitcast(I32), 0)
@@ -91,11 +92,10 @@ def tile_picked_zeropt_none_l_kernel(tc, xT, zp, csum, w1_words, w1_scales, offs
             )
         load_pair(2)
         load_plane(2)
-        load_words(0)
         load_plane(3)
         load_words(1)
 
-        zp_window = keep.tile([P, T], F32, name="zp_window", tag="zp_window_then_picked0")
+        zp_window = keep.tile([P, T], F32, name="zp_window", tag="zp_window_then_picked0", align_bytes=64)
         zp_view = zp_window[:].rearrange("p (n m) -> p n m", m=ZP_COLS)
         for bank in range(SPREAD_BANKS):
             spread = psum.tile([P, SPREADS_PER_BANK, P], F32, name=f"spread_{bank}", tag=f"bank_{bank}")
@@ -131,10 +131,21 @@ def tile_picked_zeropt_none_l_kernel(tc, xT, zp, csum, w1_words, w1_scales, offs
         def entries(lo, hi):
             return offsets[:, lo // ENTRIES_PER_COLUMN : hi // ENTRIES_PER_COLUMN]
 
-        picked0 = keep.tile([P, 2 * S], U32, name="picked0", tag="zp_window_then_picked0")
-        picked0_view = picked0[:].rearrange("p (u h s) -> p u h s", h=2, s=HALF_S)
+        pass0 = keep.tile([P, 2 * S], U32, name="pass0", tag="zp_window_then_picked0", align_bytes=64)
+        picked0 = pass0[:, 0:S].rearrange("p (h s) -> p h s", h=2)
+        woven0 = [
+            keep.tile([P, HALF_S, 2], U32, name="woven0", align_bytes=64)[:],
+            pass0[:, S : 2 * S].rearrange("p (s h) -> p s h", h=2),
+        ]
+        codes0 = keep.tile([P, S], U32, name="codes0", align_bytes=64)
+        scales0 = keep.tile([P, S], U8, name="scales0", align_bytes=64)
+
+        def gather0(h):
+            nc.vector.tensor_copy(picked0[:, h, :], window(h).indirect(entries(0, HALF_S)))
+            nc.vector.tensor_copy(woven0[1][:, :, h], window(h).indirect(entries(HALF_S, S)))
+
         round_pair(0)
-        nc.vector.tensor_copy(picked0_view[:, :, 0, :], window(0).indirect(offsets[:]))
+        gather0(0)
 
         csum_cols = psum.tile([P, P], F32, name="csum_cols", tag="bank_4")
         nc.tensor.transpose(csum_cols[:], csum_rows[:], ident[:])
@@ -142,24 +153,19 @@ def tile_picked_zeropt_none_l_kernel(tc, xT, zp, csum, w1_words, w1_scales, offs
         nc.scalar.activation(neg_csum[:], csum_cols[:, 0:BLOCKS], COPY, scale=-1.0)
 
         round_pair(1)
-        for u in range(2):
-            nc.vector.tensor_copy(picked0_view[:, u, 1, :], window(1).indirect(entries(u * HALF_S, (u + 1) * HALF_S)))
-        woven0 = [keep.tile([P, HALF_S, 2], I32, name=f"woven0_{u}", align_bytes=64) for u in range(2)]
-        codes0 = keep.tile([P, S], U32, name="codes0", align_bytes=64)
-        scales0 = keep.tile([P, S], U8, name="scales0", align_bytes=64)
-        nc.scalar.copy(woven0[0][:].bitcast(U32), picked0_view[:, 0, :, :].rearrange("p h s -> p s h"))
-        nc.vector.tensor_copy(woven0[1][:], picked0_view[:, 1, :, :].bitcast(I32).rearrange("p h s -> p s h"))
+        gather0(1)
+        nc.scalar.copy(woven0[0], picked0.rearrange("p h s -> p s h"))
 
         def quantise0(u):
             nc.vector.quantize_mx(
                 out=codes0[:, u * HALF_S : (u + 1) * HALF_S].bitcast(FP8X4),
                 scales=scales0[:, u * HALF_S : (u + 1) * HALF_S],
-                in_=woven0[u][:].rearrange("p s h -> p (s h)").bitcast(BF16),
+                in_=woven0[u].rearrange("p s h -> p (s h)").bitcast(BF16),
             )
 
+        quantise0(0)
         quantise0(1)
         round_pair(2)
-        quantise0(0)
 
         sums = {}
         for c in range(CHUNKS):
@@ -185,28 +191,35 @@ def tile_picked_zeropt_none_l_kernel(tc, xT, zp, csum, w1_words, w1_scales, offs
         woven1 = keep.tile([P, 4 * S], BF16, name="woven1", align_bytes=64)
         woven1_words = woven1[:].bitcast(U32).rearrange("p (s h) -> p s h", h=2)
         woven1_slots = woven1[:].rearrange("p (s t) -> p s t", t=4)
-        for lo, hi in SCALAR_RUNS + [(0, CHUNK)]:
-            nc.vector.tensor_copy(woven1_words[:, lo:hi, 0], window(2).indirect(entries(lo, hi)))
+        picked1 = pairs[0][:, 0 : 4 * HALF_S]
+        picked1_words = picked1.bitcast(U32).rearrange("p (h s) -> p h s", h=2)
+        picked1_slots = picked1.rearrange("p (h s e) -> p h s e", h=2, e=2)
+        nc.vector.tensor_copy(picked1_words[:, 0, :], window(2).indirect(entries(HALF_S, S)))
+        nc.vector.tensor_copy(woven1_words[:, 0:HALF_S, 0], window(2).indirect(entries(0, HALF_S)))
 
         rounded = {t: keep.tile([P, T], BF16, name=f"rounded_{t}") for t in (2, 3)}
         nc.scalar.copy(rounded[2][:, 0:HALF_T], planes[2][:, 0:HALF_T])
         nc.scalar.copy(rounded[2][:, HALF_T:1536], planes[2][:, HALF_T:1536])
         gpsimd_round(rounded[2][:, 1536:T], planes[2][:, 1536:T])
-        for lo, hi in SCALAR_RUNS:
-            nc.scalar.activation(woven1_slots[:, lo:hi, 2], rounded[2][:].indirect(entries(lo, hi)), COPY)
-        nc.vector.tensor_copy(woven1_slots[:, 0:CHUNK, 2], planes[2][:].indirect(entries(0, CHUNK)))
-        for lo, hi in PLANE_PIECES[3]:
+        nc.scalar.activation(picked1_slots[:, 1, :, 0], rounded[2][:].indirect(entries(HALF_S, S)), COPY)
+        nc.vector.tensor_copy(woven1_slots[:, 0:HALF_S, 2], planes[2][:].indirect(entries(0, HALF_S)))
+        nc.scalar.copy(woven1_words[:, HALF_S:S, :], picked1_words.rearrange("p h s -> p s h"))
+        for lo, hi in ((0, 768), (768, 1536), (1536, 1792)):
             gpsimd_round(rounded[3][:, lo:hi], planes[3][:, lo:hi])
+        nc.scalar.copy(rounded[3][:, 1792:T], planes[3][:, 1792:T])
 
         codes1 = keep.tile([P, S], U32, name="codes1", align_bytes=64)
         scales1 = keep.tile([P, S], U8, name="scales1", align_bytes=64)
 
-        def finish(c):
+        def gather_last(c):
             lo, hi = c * CHUNK, (c + 1) * CHUNK
-            if c == 0:
+            if hi <= HALF_S:
                 nc.vector.tensor_copy(woven1_slots[:, lo:hi, 3], planes[3][:].indirect(entries(lo, hi)))
             else:
                 nc.scalar.activation(woven1_slots[:, lo:hi, 3], rounded[3][:].indirect(entries(lo, hi)), COPY)
+
+        def finish(c):
+            lo, hi = c * CHUNK, (c + 1) * CHUNK
             nc.vector.quantize_mx(
                 out=codes1[:, lo:hi].bitcast(FP8X4), scales=scales1[:, lo:hi], in_=woven1[:, 4 * lo : 4 * hi]
             )
@@ -221,8 +234,12 @@ def tile_picked_zeropt_none_l_kernel(tc, xT, zp, csum, w1_words, w1_scales, offs
                 )
                 nc.sync.dma_start(out[b * P : (b + 1) * P, columns], result[:])
 
+        for c in range(CHUNKS):
+            gather_last(c)
         finish(0)
+        finish(1)
+        finish(2)
+        store(0)
+        finish(3)
         for c in range(1, CHUNKS):
-            finish(c)
-            store(c - 1)
-        store(CHUNKS - 1)
+            store(c)

@@ -30,6 +30,7 @@ HALF_T = T // 2
 HALF_S = S // 2
 CHUNK = 256
 CHUNKS = S // CHUNK
+WOVEN = 544
 PAIRS = [(0, 0), (0, 1), (1, 0)]
 VECTOR_TOKENS = [0, 512, 256]
 GPSIMD_TOKENS = {(0, 0): 448, (1, 768): 512, (2, 1280): 768, (2, 512): 192}
@@ -38,7 +39,7 @@ PIECES = [
     [(768, T), (0, 768)],
     [(1280, T), (512, 1280), (0, 512)],
 ]
-PLANE_PIECES = {2: [(0, HALF_T), (HALF_T, T)], 3: [(0, 768), (768, 1536), (1536, T)]}
+PLANE_PIECES = {2: [(0, 1280), (1280, T)], 3: [(0, 768), (768, 1536), (1536, T)]}
 
 
 def tile_picked_zeropt_none_l_kernel(tc, xT, zp, csum, w1_words, w1_scales, offs, out):
@@ -131,18 +132,16 @@ def tile_picked_zeropt_none_l_kernel(tc, xT, zp, csum, w1_words, w1_scales, offs
         def entries(lo, hi):
             return offsets[:, lo // ENTRIES_PER_COLUMN : hi // ENTRIES_PER_COLUMN]
 
-        pass0 = keep.tile([P, 2 * S], U32, name="pass0", tag="zp_window_then_picked0", align_bytes=64)
-        picked0 = pass0[:, 0:S].rearrange("p (h s) -> p h s", h=2)
-        woven0 = [
-            keep.tile([P, HALF_S, 2], U32, name="woven0", align_bytes=64)[:],
-            pass0[:, S : 2 * S].rearrange("p (s h) -> p s h", h=2),
-        ]
+        pass0 = keep.tile([P, 2 * WOVEN + 2 * S], U32, name="pass0", tag="zp_window_then_picked0", align_bytes=64)
+        picked0 = pass0[:, 0 : 2 * WOVEN].rearrange("p (h s) -> p h s", h=2)
+        woven0 = pass0[:, 2 * WOVEN :]
+        woven0_words = woven0.rearrange("p (s h) -> p s h", h=2)
         codes0 = keep.tile([P, S], U32, name="codes0", align_bytes=64)
         scales0 = keep.tile([P, S], U8, name="scales0", align_bytes=64)
 
         def gather0(h):
-            nc.vector.tensor_copy(picked0[:, h, :], window(h).indirect(entries(0, HALF_S)))
-            nc.vector.tensor_copy(woven0[1][:, :, h], window(h).indirect(entries(HALF_S, S)))
+            nc.vector.tensor_copy(picked0[:, h, :], window(h).indirect(entries(0, WOVEN)))
+            nc.vector.tensor_copy(woven0_words[:, WOVEN:S, h], window(h).indirect(entries(WOVEN, S)))
 
         round_pair(0)
         gather0(0)
@@ -154,13 +153,13 @@ def tile_picked_zeropt_none_l_kernel(tc, xT, zp, csum, w1_words, w1_scales, offs
 
         round_pair(1)
         gather0(1)
-        nc.scalar.copy(woven0[0], picked0.rearrange("p h s -> p s h"))
+        nc.scalar.copy(woven0_words[:, 0:WOVEN, :], picked0.rearrange("p h s -> p s h"))
 
         def quantise0(u):
             nc.vector.quantize_mx(
                 out=codes0[:, u * HALF_S : (u + 1) * HALF_S].bitcast(FP8X4),
                 scales=scales0[:, u * HALF_S : (u + 1) * HALF_S],
-                in_=woven0[u].rearrange("p s h -> p (s h)").bitcast(BF16),
+                in_=woven0[:, u * S : (u + 1) * S].bitcast(BF16),
             )
 
         quantise0(0)
@@ -198,15 +197,13 @@ def tile_picked_zeropt_none_l_kernel(tc, xT, zp, csum, w1_words, w1_scales, offs
         nc.vector.tensor_copy(woven1_words[:, 0:HALF_S, 0], window(2).indirect(entries(0, HALF_S)))
 
         rounded = {t: keep.tile([P, T], BF16, name=f"rounded_{t}") for t in (2, 3)}
-        nc.scalar.copy(rounded[2][:, 0:HALF_T], planes[2][:, 0:HALF_T])
-        nc.scalar.copy(rounded[2][:, HALF_T:1536], planes[2][:, HALF_T:1536])
-        gpsimd_round(rounded[2][:, 1536:T], planes[2][:, 1536:T])
+        for copy, lo, hi in ((nc.scalar.copy, 0, 768), (gpsimd_round, 768, 1280), (nc.scalar.copy, 1280, 1728), (gpsimd_round, 1728, T)):
+            copy(rounded[2][:, lo:hi], planes[2][:, lo:hi])
         nc.scalar.activation(picked1_slots[:, 1, :, 0], rounded[2][:].indirect(entries(HALF_S, S)), COPY)
         nc.vector.tensor_copy(woven1_slots[:, 0:HALF_S, 2], planes[2][:].indirect(entries(0, HALF_S)))
         nc.scalar.copy(woven1_words[:, HALF_S:S, :], picked1_words.rearrange("p h s -> p s h"))
-        for lo, hi in ((0, 768), (768, 1536), (1536, 1792)):
+        for lo, hi in PLANE_PIECES[3]:
             gpsimd_round(rounded[3][:, lo:hi], planes[3][:, lo:hi])
-        nc.scalar.copy(rounded[3][:, 1792:T], planes[3][:, 1792:T])
 
         codes1 = keep.tile([P, S], U32, name="codes1", align_bytes=64)
         scales1 = keep.tile([P, S], U8, name="scales1", align_bytes=64)

@@ -30,7 +30,7 @@ HALF_T = T // 2
 HALF_S = S // 2
 CHUNK = 256
 CHUNKS = S // CHUNK
-WOVEN = 544
+WOVEN = 512
 PAIRS = [(0, 0), (0, 1), (1, 0)]
 VECTOR_TOKENS = [0, 512, 256]
 GPSIMD_TOKENS = {(0, 0): 448, (1, 768): 512, (2, 1280): 768, (2, 512): 192}
@@ -190,18 +190,21 @@ def tile_picked_zeropt_none_l_kernel(tc, xT, zp, csum, w1_words, w1_scales, offs
         woven1 = keep.tile([P, 4 * S], BF16, name="woven1", align_bytes=64)
         woven1_words = woven1[:].bitcast(U32).rearrange("p (s h) -> p s h", h=2)
         woven1_slots = woven1[:].rearrange("p (s t) -> p s t", t=4)
-        picked1 = pairs[0][:, 0 : 4 * HALF_S]
-        picked1_words = picked1.bitcast(U32).rearrange("p (h s) -> p h s", h=2)
-        picked1_slots = picked1.rearrange("p (h s e) -> p h s e", h=2, e=2)
-        nc.vector.tensor_copy(picked1_words[:, 0, :], window(2).indirect(entries(HALF_S, S)))
-        nc.vector.tensor_copy(woven1_words[:, 0:HALF_S, 0], window(2).indirect(entries(0, HALF_S)))
+        picked1 = pairs[0][:, 0 : 4 * (S - CHUNK)]
+        picked1_words = picked1.bitcast(U32).rearrange("p (c h s) -> p c h s", h=2, s=CHUNK)
+        picked1_slots = picked1.rearrange("p (c h s e) -> p c h s e", h=2, s=CHUNK, e=2)
+        nc.vector.tensor_copy(picked1_words[:, :, 0, :], window(2).indirect(entries(CHUNK, S)))
+        nc.vector.tensor_copy(picked1_slots[:, 0, 1, :, 0], planes[2][:].indirect(entries(CHUNK, 2 * CHUNK)))
+        nc.vector.tensor_copy(woven1_words[:, 0:CHUNK, 0], window(2).indirect(entries(0, CHUNK)))
+        nc.vector.tensor_copy(woven1_slots[:, 0:CHUNK, 2], planes[2][:].indirect(entries(0, CHUNK)))
 
         rounded = {t: keep.tile([P, T], BF16, name=f"rounded_{t}") for t in (2, 3)}
         for copy, lo, hi in ((nc.scalar.copy, 0, 768), (gpsimd_round, 768, 1280), (nc.scalar.copy, 1280, 1728), (gpsimd_round, 1728, T)):
             copy(rounded[2][:, lo:hi], planes[2][:, lo:hi])
-        nc.scalar.activation(picked1_slots[:, 1, :, 0], rounded[2][:].indirect(entries(HALF_S, S)), COPY)
-        nc.vector.tensor_copy(woven1_slots[:, 0:HALF_S, 2], planes[2][:].indirect(entries(0, HALF_S)))
-        nc.scalar.copy(woven1_words[:, HALF_S:S, :], picked1_words.rearrange("p h s -> p s h"))
+        nc.scalar.activation(picked1_slots[:, 1:3, 1, :, 0], rounded[2][:].indirect(entries(HALF_S, S)), COPY)
+        later_words = woven1_words[:, CHUNK:S, :].rearrange("p (c s) h -> p c s h", s=CHUNK)
+        for lo, hi in ((0, 2), (2, 3)):
+            nc.scalar.copy(later_words[:, lo:hi], picked1_words[:, lo:hi].rearrange("p c h s -> p c s h"))
         for lo, hi in PLANE_PIECES[3]:
             gpsimd_round(rounded[3][:, lo:hi], planes[3][:, lo:hi])
 

@@ -187,26 +187,29 @@ def tile_picked_zeropt_none_l_kernel(tc, xT, zp, csum, w1_words, w1_scales, offs
         for c in range(CHUNKS):
             multiply(0, c, codes0[:, c * CHUNK : (c + 1) * CHUNK], scales0[:, c * CHUNK : (c + 1) * CHUNK])
 
-        woven1 = keep.tile([P, 4 * S], BF16, name="woven1", align_bytes=64)
-        woven1_words = woven1[:].bitcast(U32).rearrange("p (s h) -> p s h", h=2)
-        woven1_slots = woven1[:].rearrange("p (s t) -> p s t", t=4)
+        rounded = {t: keep.tile([P, T], BF16, name=f"rounded_{t}", align_bytes=64) for t in (2, 3)}
+        woven1 = [keep.tile([P, 4 * CHUNK], BF16, name=f"woven1_{c}", align_bytes=64)[:] for c in (0, 2, 3)]
+        woven1 = [woven1[0], rounded[2][:, 0 : 4 * CHUNK], woven1[1], woven1[2]]
+        woven1_words = [w.bitcast(U32).rearrange("p (s h) -> p s h", h=2) for w in woven1]
+        woven1_slots = [w.rearrange("p (s t) -> p s t", t=4) for w in woven1]
         picked1 = pairs[0][:, 0 : 4 * (S - CHUNK)]
         picked1_words = picked1.bitcast(U32).rearrange("p (c h s) -> p c h s", h=2, s=CHUNK)
         picked1_slots = picked1.rearrange("p (c h s e) -> p c h s e", h=2, s=CHUNK, e=2)
         nc.vector.tensor_copy(picked1_words[:, :, 0, :], window(2).indirect(entries(CHUNK, S)))
         nc.vector.tensor_copy(picked1_slots[:, 0, 1, :, 0], planes[2][:].indirect(entries(CHUNK, 2 * CHUNK)))
-        nc.vector.tensor_copy(woven1_words[:, 0:CHUNK, 0], window(2).indirect(entries(0, CHUNK)))
-        nc.vector.tensor_copy(woven1_slots[:, 0:CHUNK, 2], planes[2][:].indirect(entries(0, CHUNK)))
+        nc.vector.tensor_copy(woven1_words[0][:, :, 0], window(2).indirect(entries(0, CHUNK)))
+        nc.vector.tensor_copy(woven1_slots[0][:, :, 2], planes[2][:].indirect(entries(0, CHUNK)))
 
-        rounded = {t: keep.tile([P, T], BF16, name=f"rounded_{t}") for t in (2, 3)}
         for copy, lo, hi in ((nc.scalar.copy, 0, 768), (gpsimd_round, 768, 1280), (nc.scalar.copy, 1280, 1728), (gpsimd_round, 1728, T)):
             copy(rounded[2][:, lo:hi], planes[2][:, lo:hi])
         nc.scalar.activation(picked1_slots[:, 1:3, 1, :, 0], rounded[2][:].indirect(entries(HALF_S, S)), COPY)
-        later_words = woven1_words[:, CHUNK:S, :].rearrange("p (c s) h -> p c s h", s=CHUNK)
-        for lo, hi in ((0, 2), (2, 3)):
-            nc.scalar.copy(later_words[:, lo:hi], picked1_words[:, lo:hi].rearrange("p c h s -> p c s h"))
-        for lo, hi in PLANE_PIECES[3]:
-            gpsimd_round(rounded[3][:, lo:hi], planes[3][:, lo:hi])
+
+        def weave(c):
+            nc.scalar.copy(woven1_words[c], picked1_words[:, c - 1].rearrange("p h s -> p s h"))
+
+        weave(1)
+        for copy, lo, hi in ((gpsimd_round, 0, 768), (gpsimd_round, 768, 1536), (gpsimd_round, 1536, 1792), (nc.scalar.copy, 1792, T)):
+            copy(rounded[3][:, lo:hi], planes[3][:, lo:hi])
 
         codes1 = keep.tile([P, S], U32, name="codes1", align_bytes=64)
         scales1 = keep.tile([P, S], U8, name="scales1", align_bytes=64)
@@ -214,14 +217,14 @@ def tile_picked_zeropt_none_l_kernel(tc, xT, zp, csum, w1_words, w1_scales, offs
         def gather_last(c):
             lo, hi = c * CHUNK, (c + 1) * CHUNK
             if hi <= HALF_S:
-                nc.vector.tensor_copy(woven1_slots[:, lo:hi, 3], planes[3][:].indirect(entries(lo, hi)))
+                nc.vector.tensor_copy(woven1_slots[c][:, :, 3], planes[3][:].indirect(entries(lo, hi)))
             else:
-                nc.scalar.activation(woven1_slots[:, lo:hi, 3], rounded[3][:].indirect(entries(lo, hi)), COPY)
+                nc.scalar.activation(picked1_slots[:, c - 1, 1, :, 1], rounded[3][:].indirect(entries(lo, hi)), COPY)
 
         def finish(c):
             lo, hi = c * CHUNK, (c + 1) * CHUNK
             nc.vector.quantize_mx(
-                out=codes1[:, lo:hi].bitcast(FP8X4), scales=scales1[:, lo:hi], in_=woven1[:, 4 * lo : 4 * hi]
+                out=codes1[:, lo:hi].bitcast(FP8X4), scales=scales1[:, lo:hi], in_=woven1[c]
             )
             multiply(1, c, codes1[:, lo:hi], scales1[:, lo:hi])
 
@@ -236,6 +239,8 @@ def tile_picked_zeropt_none_l_kernel(tc, xT, zp, csum, w1_words, w1_scales, offs
 
         for c in range(CHUNKS):
             gather_last(c)
+        for c in range(2, CHUNKS):
+            weave(c)
         finish(0)
         finish(1)
         finish(2)

@@ -19,27 +19,17 @@ ADD = mybir.AluOpType.add
 COPY = mybir.ActivationFunctionType.Copy
 
 P = 128
-PASSES = K // (4 * P)
+SLOTS = 4
+PASSES = K // (SLOTS * P)
 BLOCKS = N // P
 ENTRIES_PER_COLUMN = 16
 SCALE_ROWS = 4
 ZP_COLS = T // P
 SPREADS_PER_BANK = 4
 SPREAD_BANKS = ZP_COLS // SPREADS_PER_BANK
-HALF_T = T // 2
-HALF_S = S // 2
 CHUNK = 256
 CHUNKS = S // CHUNK
-WOVEN = 512
-PAIRS = [(0, 0), (0, 1), (1, 0)]
-VECTOR_TOKENS = [0, 512, 256]
-GPSIMD_TOKENS = {(0, 0): 448, (1, 768): 512, (2, 1280): 768, (2, 512): 192}
-PIECES = [
-    [(HALF_T, T), (0, HALF_T)],
-    [(768, T), (0, 768)],
-    [(1280, T), (512, 1280), (0, 512)],
-]
-PLANE_PIECES = {2: [(0, 1280), (1280, T)], 3: [(0, 768), (768, 1536), (1536, T)]}
+HALF = S // 2
 
 
 def tile_picked_zeropt_none_l_kernel(tc, xT, zp, csum, w1_words, w1_scales, offs, out):
@@ -48,55 +38,44 @@ def tile_picked_zeropt_none_l_kernel(tc, xT, zp, csum, w1_words, w1_scales, offs
         keep = ctx.enter_context(tc.tile_pool(name="keep", bufs=1))
         psum = ctx.enter_context(tc.psum_pool(name="psum", bufs=1))
 
-        offsets = keep.tile([P, S // ENTRIES_PER_COLUMN], U16, name="offsets")
         zp_rows = keep.tile([P, ZP_COLS], F32, name="zp_rows")
         nc.sync.dma_start(zp_rows[:], zp[0, :].rearrange("(n m) -> n m", m=ZP_COLS))
+        offsets = keep.tile([P, S // ENTRIES_PER_COLUMN], U16, name="offsets")
+        nc.sync.dma_start(offsets[:], offs)
 
-        x_rows = xT.rearrange("(z p h e) t -> z h p e t", z=PASSES, p=P, h=2, e=2)
-        raw = {}
-
-        def load_pair(i):
-            z, h = PAIRS[i]
-            for lo, hi in PIECES[i]:
-                piece = keep.tile([P, 2, hi - lo], F32, name=f"raw_{i}_{lo}")[:]
-                nc.sync.dma_start(piece, x_rows[z, h, :, :, lo:hi])
-                raw[i, lo] = piece
-                if (i, lo) == (0, HALF_T):
-                    nc.sync.dma_start(offsets[:], offs)
-
-        planes = {t: keep.tile([P, T], F32, name=f"plane_{t}") for t in (2, 3)}
-
-        def load_plane(t):
-            for lo, hi in PLANE_PIECES[t]:
-                nc.sync.dma_start(planes[t][:, lo:hi], x_rows[1, 1, :, t - 2, lo:hi])
-                if (t, lo) == (3, 0):
-                    load_words(0)
-
-        w_scales = keep.tile([P, N], U8, name="w_scales", align_bytes=64)
-        nc.gpsimd.memset(w_scales[:].bitcast(I32), 0)
+        w_scales = [keep.tile([P, N], U8, name=f"w_scales_{z}", align_bytes=64) for z in range(PASSES)]
+        for z in range(PASSES):
+            nc.gpsimd.memset(w_scales[z][:].bitcast(I32), 0)
         ident = keep.tile([P, P], F32, name="ident")
         make_identity(nc, ident[:])
         csum_rows = keep.tile([P, P], F32, name="csum_rows")
         nc.gpsimd.memset(csum_rows[:], 0.0)
         w_words = [keep.tile([P, N], U32, name=f"w_words_{z}", align_bytes=64) for z in range(PASSES)]
 
-        def load_words(z):
+        def load_weights(z):
+            for q in range(P // 32):
+                nc.sync.dma_start(
+                    w_scales[z][32 * q : 32 * q + SCALE_ROWS, :].bitcast(I32),
+                    w1_scales[z, SCALE_ROWS * q : SCALE_ROWS * (q + 1), :].bitcast(I32),
+                )
             nc.sync.dma_start(w_words[z][:].bitcast(I32), w1_words[z].rearrange("p n t -> p (n t)").bitcast(I32))
 
-        load_pair(0)
-        nc.sync.dma_start(csum_rows[0:BLOCKS, :], csum.rearrange("(b p) o -> b (p o)", p=P))
-        load_pair(1)
-        for q in range(P // 32):
-            nc.sync.dma_start(
-                w_scales[32 * q : 32 * q + SCALE_ROWS * PASSES, :].bitcast(I32),
-                w1_scales[:, SCALE_ROWS * q : SCALE_ROWS * (q + 1), :].bitcast(I32),
-            )
-        load_pair(2)
-        load_plane(2)
-        load_plane(3)
-        load_words(1)
+        x_rows = xT.rearrange("(z p t) n -> z t p n", z=PASSES, p=P, t=SLOTS)
+        planes = {}
+        for z in range(PASSES):
+            for t in range(SLOTS):
+                if (z, t) == (PASSES - 1, SLOTS - 1):
+                    load_weights(0)
+                planes[z, t] = keep.tile([P, T], F32, name=f"plane_{z}_{t}")
+                nc.sync.dma_start(planes[z, t][:], x_rows[z, t])
+                if (z, t) == (0, 0):
+                    nc.sync.dma_start(csum_rows[0:BLOCKS, :], csum.rearrange("(b p) o -> b (p o)", p=P))
+        load_weights(1)
 
-        zp_window = keep.tile([P, T], F32, name="zp_window", tag="zp_window_then_picked0", align_bytes=64)
+        def entries(lo, hi):
+            return offsets[:, lo // ENTRIES_PER_COLUMN : hi // ENTRIES_PER_COLUMN]
+
+        zp_window = keep.tile([P, T], F32, name="zp_window", tag="zp_window_then_pass0", align_bytes=64)
         zp_view = zp_window[:].rearrange("p (n m) -> p n m", m=ZP_COLS)
         for bank in range(SPREAD_BANKS):
             spread = psum.tile([P, SPREADS_PER_BANK, P], F32, name=f"spread_{bank}", tag=f"bank_{bank}")
@@ -104,67 +83,37 @@ def tile_picked_zeropt_none_l_kernel(tc, xT, zp, csum, w1_words, w1_scales, offs
             for i in range(SPREADS_PER_BANK):
                 column = zp_rows[:, first_m + i : first_m + i + 1]
                 nc.tensor.transpose(spread[:, i, :], column.to_broadcast([P, P]), ident[:])
-            nc.vector.tensor_copy(
-                zp_view[:, :, first_m : first_m + SPREADS_PER_BANK], spread[:].rearrange("p i n -> p n i")
-            )
-        zp_picked = keep.tile([P, S], F32, name="zp_picked")
-        nc.vector.tensor_copy(zp_picked[:], zp_window[:].indirect(offsets[:]))
-
-        pairs = [keep.tile([P, 2 * T], BF16, name=f"pair_{i}") for i in range(len(PAIRS))]
-
-        def gpsimd_round(rounded, values):
-            nc.gpsimd.tensor_scalar(rounded, values, 1.0, 0.0, MULT, ADD)
-
-        def round_pair(i):
-            for lo, hi in PIECES[i]:
-                cut = min(max(VECTOR_TOKENS[i], lo), hi)
-                side = cut + GPSIMD_TOKENS.get((i, lo), 0)
-                for copy, a, b in ((nc.scalar.copy, side, hi), (gpsimd_round, cut, side), (nc.vector.tensor_copy, lo, cut)):
-                    if a < b:
-                        copy(
-                            pairs[i][:, 2 * a : 2 * b].rearrange("p (c e) -> p c e", e=2),
-                            raw[i, lo][:, :, a - lo : b - lo].rearrange("p e c -> p c e"),
-                        )
-
-        def window(i):
-            return pairs[i][:].bitcast(U32)
-
-        def entries(lo, hi):
-            return offsets[:, lo // ENTRIES_PER_COLUMN : hi // ENTRIES_PER_COLUMN]
-
-        pass0 = keep.tile([P, 2 * WOVEN + 2 * S], U32, name="pass0", tag="zp_window_then_picked0", align_bytes=64)
-        picked0 = pass0[:, 0 : 2 * WOVEN].rearrange("p (h s) -> p h s", h=2)
-        woven0 = pass0[:, 2 * WOVEN :]
-        woven0_words = woven0.rearrange("p (s h) -> p s h", h=2)
-        codes0 = keep.tile([P, S], U32, name="codes0", align_bytes=64)
-        scales0 = keep.tile([P, S], U8, name="scales0", align_bytes=64)
-
-        def gather0(h):
-            nc.vector.tensor_copy(picked0[:, h, :], window(h).indirect(entries(0, WOVEN)))
-            nc.vector.tensor_copy(woven0_words[:, WOVEN:S, h], window(h).indirect(entries(WOVEN, S)))
-
-        round_pair(0)
-        gather0(0)
+            copy = nc.vector.tensor_copy if bank % 2 == 0 else nc.scalar.copy
+            copy(zp_view[:, :, first_m : first_m + SPREADS_PER_BANK], spread[:].rearrange("p i n -> p n i"))
+        zp_low = [
+            keep.tile([P, CHUNK], F32, name=f"zp_low_{c}", tag=f"zp_then_codes_{c}", align_bytes=64) for c in range(2)
+        ]
+        zp_high = keep.tile([P, HALF], F32, name="zp_high")
+        for c in range(2):
+            nc.vector.tensor_copy(zp_low[c][:], zp_window[:].indirect(entries(c * CHUNK, (c + 1) * CHUNK)))
+        nc.scalar.activation(zp_high[:], zp_window[:].indirect(entries(HALF, S)), COPY)
+        zp_picked = [zp_low[0][:], zp_low[1][:], zp_high[:, 0:CHUNK], zp_high[:, CHUNK:HALF]]
 
         csum_cols = psum.tile([P, P], F32, name="csum_cols", tag="bank_4")
         nc.tensor.transpose(csum_cols[:], csum_rows[:], ident[:])
         neg_csum = keep.tile([P, BLOCKS], F32, name="neg_csum")
         nc.scalar.activation(neg_csum[:], csum_cols[:, 0:BLOCKS], COPY, scale=-1.0)
 
-        round_pair(1)
-        gather0(1)
-        nc.scalar.copy(woven0_words[:, 0:WOVEN, :], picked0.rearrange("p h s -> p s h"))
+        pass0 = keep.tile([P, 2 * SLOTS * HALF], BF16, name="pass0", tag="zp_window_then_pass0", align_bytes=64)
+        picked_rows = pass0[:, SLOTS * HALF :].rearrange("p (t s) -> p t s", t=SLOTS)
 
-        def quantise0(u):
-            nc.vector.quantize_mx(
-                out=codes0[:, u * HALF_S : (u + 1) * HALF_S].bitcast(FP8X4),
-                scales=scales0[:, u * HALF_S : (u + 1) * HALF_S],
-                in_=woven0[:, u * S : (u + 1) * S].bitcast(BF16),
-            )
+        def slots(woven):
+            return woven.rearrange("p (s t) -> p s t", t=SLOTS)
 
-        quantise0(0)
-        quantise0(1)
-        round_pair(2)
+        def gather_direct(woven, z, t, lo, hi):
+            nc.vector.tensor_copy(slots(woven)[:, :, t], planes[z, t][:].indirect(entries(lo, hi)))
+
+        def gather_plain(target, z, t, lo, hi):
+            nc.scalar.activation(target, planes[z, t][:].indirect(entries(lo, hi)), COPY)
+
+        def weave(copy, woven, c):
+            lo = c * CHUNK - HALF
+            copy(slots(woven), picked_rows[:, :, lo : lo + CHUNK].rearrange("p t s -> p s t"))
 
         sums = {}
         for c in range(CHUNKS):
@@ -177,74 +126,82 @@ def tile_picked_zeropt_none_l_kernel(tc, xT, zp, csum, w1_words, w1_scales, offs
                 nc.tensor.matmul_mx(
                     out=sums[c, b][:],
                     lhsT=w_words[z][:, channels].bitcast(FP8X4),
-                    lhsT_scale=w_scales[SCALE_ROWS * z : P, channels],
+                    lhsT_scale=w_scales[z][:, channels],
                     rhs=codes.bitcast(FP8X4),
                     rhs_scale=scales,
                     start=(z == 0),
                     stop=(z == PASSES - 1),
                 )
 
+        woven0_high = keep.tile([P, SLOTS * HALF], BF16, name="woven0_high", align_bytes=64)
+        woven0 = [pass0[:, 0 : SLOTS * HALF], woven0_high[:]]
+        codes0 = keep.tile([P, S], U32, name="codes0", align_bytes=64)
+        scales0 = keep.tile([P, S], U8, name="scales0", align_bytes=64)
+
+        def quantise0(u):
+            columns = slice(u * HALF, (u + 1) * HALF)
+            nc.vector.quantize_mx(out=codes0[:, columns].bitcast(FP8X4), scales=scales0[:, columns], in_=woven0[u])
+
+        for t in range(SLOTS):
+            gather_direct(woven0[0], 0, t, 0, HALF)
+            gather_plain(picked_rows[:, t, :], 0, t, HALF, S)
+        for c in (2, 3):
+            weave(nc.scalar.copy, woven0[1][:, (c - 2) * SLOTS * CHUNK : (c - 1) * SLOTS * CHUNK], c)
+        quantise0(0)
+
+        woven1_low = keep.tile([P, SLOTS * HALF], BF16, name="woven1_low", align_bytes=64)
+        woven1 = [woven1_low[:, 0 : SLOTS * CHUNK], woven1_low[:, SLOTS * CHUNK :]]
+        woven1.extend(keep.tile([P, SLOTS * CHUNK], BF16, name=f"woven1_{c}", align_bytes=64)[:] for c in (2, 3))
+        for t in range(SLOTS - 1):
+            gather_direct(woven1_low[:], 1, t, 0, HALF)
+            gather_plain(picked_rows[:, t, :], 1, t, HALF, S)
+            if t == 1:
+                quantise0(1)
+        weave(nc.scalar.copy, woven1[2], 2)
+        weave(nc.vector.tensor_copy, woven1[3], 3)
         for c in range(CHUNKS):
             multiply(0, c, codes0[:, c * CHUNK : (c + 1) * CHUNK], scales0[:, c * CHUNK : (c + 1) * CHUNK])
 
-        rounded = {t: keep.tile([P, T], BF16, name=f"rounded_{t}", align_bytes=64) for t in (2, 3)}
-        woven1 = [keep.tile([P, 4 * CHUNK], BF16, name=f"woven1_{c}", align_bytes=64)[:] for c in (0, 2, 3)]
-        woven1 = [woven1[0], rounded[2][:, 0 : 4 * CHUNK], woven1[1], woven1[2]]
-        woven1_words = [w.bitcast(U32).rearrange("p (s h) -> p s h", h=2) for w in woven1]
-        woven1_slots = [w.rearrange("p (s t) -> p s t", t=4) for w in woven1]
-        picked1 = pairs[0][:, 0 : 4 * (S - CHUNK)]
-        picked1_words = picked1.bitcast(U32).rearrange("p (c h s) -> p c h s", h=2, s=CHUNK)
-        picked1_slots = picked1.rearrange("p (c h s e) -> p c h s e", h=2, s=CHUNK, e=2)
-        nc.vector.tensor_copy(picked1_words[:, :, 0, :], window(2).indirect(entries(CHUNK, S)))
-        nc.vector.tensor_copy(picked1_slots[:, 0, 1, :, 0], planes[2][:].indirect(entries(CHUNK, 2 * CHUNK)))
-        nc.vector.tensor_copy(woven1_words[0][:, :, 0], window(2).indirect(entries(0, CHUNK)))
-        nc.vector.tensor_copy(woven1_slots[0][:, :, 2], planes[2][:].indirect(entries(0, CHUNK)))
-
-        for copy, lo, hi in ((nc.scalar.copy, 0, 768), (gpsimd_round, 768, 1280), (nc.scalar.copy, 1280, 1728), (gpsimd_round, 1728, T)):
-            copy(rounded[2][:, lo:hi], planes[2][:, lo:hi])
-        nc.scalar.activation(picked1_slots[:, 1:3, 1, :, 0], rounded[2][:].indirect(entries(HALF_S, S)), COPY)
-
-        def weave(c):
-            nc.scalar.copy(woven1_words[c], picked1_words[:, c - 1].rearrange("p h s -> p s h"))
-
-        weave(1)
-        for copy, lo, hi in ((gpsimd_round, 0, 768), (gpsimd_round, 768, 1536), (gpsimd_round, 1536, 1792), (nc.scalar.copy, 1792, T)):
-            copy(rounded[3][:, lo:hi], planes[3][:, lo:hi])
-
-        codes1 = keep.tile([P, S], U32, name="codes1", align_bytes=64)
+        last = SLOTS - 1
+        last_picked = keep.tile([P, S - CHUNK], BF16, name="last_picked")
+        codes1_low = keep.tile([P, HALF], U32, name="codes1_low", align_bytes=64)
         scales1 = keep.tile([P, S], U8, name="scales1", align_bytes=64)
 
-        def gather_last(c):
-            lo, hi = c * CHUNK, (c + 1) * CHUNK
-            if hi <= HALF_S:
-                nc.vector.tensor_copy(woven1_slots[c][:, :, 3], planes[3][:].indirect(entries(lo, hi)))
-            else:
-                nc.scalar.activation(picked1_slots[:, c - 1, 1, :, 1], rounded[3][:].indirect(entries(lo, hi)), COPY)
+        def place(copy, c):
+            copy(slots(woven1[c])[:, :, last], last_picked[:, (c - 1) * CHUNK : c * CHUNK])
 
         def finish(c):
             lo, hi = c * CHUNK, (c + 1) * CHUNK
-            nc.vector.quantize_mx(
-                out=codes1[:, lo:hi].bitcast(FP8X4), scales=scales1[:, lo:hi], in_=woven1[c]
-            )
-            multiply(1, c, codes1[:, lo:hi], scales1[:, lo:hi])
+            if hi <= HALF:
+                codes = codes1_low[:, lo:hi]
+            else:
+                codes = keep.tile([P, CHUNK], U32, name=f"codes1_{c}", tag=f"zp_then_codes_{c - 2}", align_bytes=64)[:]
+            nc.vector.quantize_mx(out=codes.bitcast(FP8X4), scales=scales1[:, lo:hi], in_=woven1[c])
+            multiply(1, c, codes, scales1[:, lo:hi])
 
-        def store(c):
+        def store(c, b):
             columns = slice(c * CHUNK, (c + 1) * CHUNK)
-            for b in range(BLOCKS):
-                result = keep.tile([P, CHUNK], F32, name=f"result_{c}_{b}")
-                nc.vector.scalar_tensor_tensor(
-                    result[:], zp_picked[:, columns], neg_csum[:, b : b + 1], sums[c, b][:], MULT, ADD
-                )
-                nc.sync.dma_start(out[b * P : (b + 1) * P, columns], result[:])
+            result = keep.tile([P, CHUNK], F32, name=f"result_{c}_{b}")
+            nc.vector.scalar_tensor_tensor(
+                result[:], zp_picked[c], neg_csum[:, b : b + 1], sums[c, b][:], MULT, ADD
+            )
+            nc.sync.dma_start(out[b * P : (b + 1) * P, columns], result[:])
 
-        for c in range(CHUNKS):
-            gather_last(c)
-        for c in range(2, CHUNKS):
-            weave(c)
+        gather_direct(woven1[0], 1, last, 0, CHUNK)
+        for c in range(1, CHUNKS):
+            gather_plain(last_picked[:, (c - 1) * CHUNK : c * CHUNK], 1, last, c * CHUNK, (c + 1) * CHUNK)
+        place(nc.vector.tensor_copy, 1)
+        place(nc.scalar.copy, 2)
+        place(nc.scalar.copy, 3)
         finish(0)
         finish(1)
+        store(0, 0)
+        store(0, 1)
+        store(1, 0)
         finish(2)
-        store(0)
+        store(1, 1)
+        store(2, 0)
         finish(3)
-        for c in range(1, CHUNKS):
-            store(c)
+        store(2, 1)
+        store(3, 0)
+        store(3, 1)

@@ -30,6 +30,8 @@ SPREAD_BANKS = ZP_COLS // SPREADS_PER_BANK
 CHUNK = 256
 CHUNKS = S // CHUNK
 HALF = S // 2
+DIRECT = [384, 512]
+GPSIMD_WEAVES = [512, 320]
 
 
 def tile_picked_zeropt_none_l_kernel(tc, xT, zp, csum, w1_words, w1_scales, offs, out):
@@ -38,7 +40,7 @@ def tile_picked_zeropt_none_l_kernel(tc, xT, zp, csum, w1_words, w1_scales, offs
         keep = ctx.enter_context(tc.tile_pool(name="keep", bufs=1))
         psum = ctx.enter_context(tc.psum_pool(name="psum", bufs=1))
 
-        zp_rows = keep.tile([P, ZP_COLS], F32, name="zp_rows")
+        zp_rows = keep.tile([P, ZP_COLS], F32, name="zp_rows", tag="zp_rows_then_picked0")
         nc.sync.dma_start(zp_rows[:], zp[0, :].rearrange("(n m) -> n m", m=ZP_COLS))
         offsets = keep.tile([P, S // ENTRIES_PER_COLUMN], U16, name="offsets")
         nc.sync.dma_start(offsets[:], offs)
@@ -89,18 +91,20 @@ def tile_picked_zeropt_none_l_kernel(tc, xT, zp, csum, w1_words, w1_scales, offs
             keep.tile([P, CHUNK], F32, name=f"zp_low_{c}", tag=f"zp_then_codes_{c}", align_bytes=64) for c in range(2)
         ]
         zp_high = keep.tile([P, HALF], F32, name="zp_high")
-        for c in range(2):
-            nc.vector.tensor_copy(zp_low[c][:], zp_window[:].indirect(entries(c * CHUNK, (c + 1) * CHUNK)))
-        nc.scalar.activation(zp_high[:], zp_window[:].indirect(entries(HALF, S)), COPY)
         zp_picked = [zp_low[0][:], zp_low[1][:], zp_high[:, 0:CHUNK], zp_high[:, CHUNK:HALF]]
+        for c in range(CHUNKS - 1):
+            nc.vector.tensor_copy(zp_picked[c], zp_window[:].indirect(entries(c * CHUNK, (c + 1) * CHUNK)))
+        nc.scalar.activation(zp_picked[CHUNKS - 1], zp_window[:].indirect(entries(S - CHUNK, S)), COPY)
 
         csum_cols = psum.tile([P, P], F32, name="csum_cols", tag="bank_4")
         nc.tensor.transpose(csum_cols[:], csum_rows[:], ident[:])
         neg_csum = keep.tile([P, BLOCKS], F32, name="neg_csum")
         nc.scalar.activation(neg_csum[:], csum_cols[:, 0:BLOCKS], COPY, scale=-1.0)
 
-        pass0 = keep.tile([P, 2 * SLOTS * HALF], BF16, name="pass0", tag="zp_window_then_pass0", align_bytes=64)
-        picked_rows = pass0[:, SLOTS * HALF :].rearrange("p (t s) -> p t s", t=SLOTS)
+        picked0 = keep.tile([P, SLOTS * (S - DIRECT[0])], BF16, name="picked0", tag="zp_rows_then_picked0")
+        picked1 = keep.tile([P, SLOTS * (S - DIRECT[1])], BF16, name="picked1")
+        nc.gpsimd.memset(picked1[:, (SLOTS - 1) * (S - DIRECT[1]) :].bitcast(I32), 0)
+        picked_rows = [tile[:].rearrange("p (t s) -> p t s", t=SLOTS) for tile in (picked0, picked1)]
 
         def slots(woven):
             return woven.rearrange("p (s t) -> p s t", t=SLOTS)
@@ -111,9 +115,16 @@ def tile_picked_zeropt_none_l_kernel(tc, xT, zp, csum, w1_words, w1_scales, offs
         def gather_plain(target, z, t, lo, hi):
             nc.scalar.activation(target, planes[z, t][:].indirect(entries(lo, hi)), COPY)
 
-        def weave(copy, woven, c):
-            lo = c * CHUNK - HALF
-            copy(slots(woven), picked_rows[:, :, lo : lo + CHUNK].rearrange("p t s -> p s t"))
+        def gpsimd_copy(target, values):
+            nc.gpsimd.tensor_scalar(target, values, 1.0, 0.0, MULT, ADD)
+
+        def gather_and_weave(woven, z, t):
+            first = DIRECT[z]
+            cut = GPSIMD_WEAVES[z]
+            for copy, lo, hi in ((gpsimd_copy, 0, cut), (nc.scalar.copy, cut, S - first)):
+                gather_plain(picked_rows[z][:, t, lo:hi], z, t, first + lo, first + hi)
+            for copy, lo, hi in ((gpsimd_copy, 0, cut), (nc.scalar.copy, cut, S - first)):
+                copy(slots(woven)[:, lo:hi, :], picked_rows[z][:, :, lo:hi].rearrange("p t s -> p s t"))
 
         sums = {}
         for c in range(CHUNKS):
@@ -133,32 +144,26 @@ def tile_picked_zeropt_none_l_kernel(tc, xT, zp, csum, w1_words, w1_scales, offs
                     stop=(z == PASSES - 1),
                 )
 
-        woven0_high = keep.tile([P, SLOTS * HALF], BF16, name="woven0_high", align_bytes=64)
-        woven0 = [pass0[:, 0 : SLOTS * HALF], woven0_high[:]]
+        woven0 = keep.tile([P, SLOTS * S], BF16, name="woven0", tag="zp_window_then_pass0", align_bytes=64)
         codes0 = keep.tile([P, S], U32, name="codes0", align_bytes=64)
         scales0 = keep.tile([P, S], U8, name="scales0", align_bytes=64)
 
-        def quantise0(u):
-            columns = slice(u * HALF, (u + 1) * HALF)
-            nc.vector.quantize_mx(out=codes0[:, columns].bitcast(FP8X4), scales=scales0[:, columns], in_=woven0[u])
-
         for t in range(SLOTS):
-            gather_direct(woven0[0], 0, t, 0, HALF)
-            gather_plain(picked_rows[:, t, :], 0, t, HALF, S)
-        for c in (2, 3):
-            weave(nc.scalar.copy, woven0[1][:, (c - 2) * SLOTS * CHUNK : (c - 1) * SLOTS * CHUNK], c)
-        quantise0(0)
+            gather_direct(woven0[:, 0 : SLOTS * DIRECT[0]], 0, t, 0, DIRECT[0])
+            if t < SLOTS - 1:
+                gather_plain(picked_rows[0][:, t, :], 0, t, DIRECT[0], S)
+        gather_and_weave(woven0[:, SLOTS * DIRECT[0] :], 0, SLOTS - 1)
 
         woven1_low = keep.tile([P, SLOTS * HALF], BF16, name="woven1_low", align_bytes=64)
-        woven1 = [woven1_low[:, 0 : SLOTS * CHUNK], woven1_low[:, SLOTS * CHUNK :]]
-        woven1.extend(keep.tile([P, SLOTS * CHUNK], BF16, name=f"woven1_{c}", align_bytes=64)[:] for c in (2, 3))
+        woven1_high = keep.tile([P, SLOTS * HALF], BF16, name="woven1_high", align_bytes=64)
+        woven1 = [w[:, u * SLOTS * CHUNK : (u + 1) * SLOTS * CHUNK] for w in (woven1_low, woven1_high) for u in range(2)]
         for t in range(SLOTS - 1):
             gather_direct(woven1_low[:], 1, t, 0, HALF)
-            gather_plain(picked_rows[:, t, :], 1, t, HALF, S)
-            if t == 1:
-                quantise0(1)
-        weave(nc.scalar.copy, woven1[2], 2)
-        weave(nc.vector.tensor_copy, woven1[3], 3)
+            if t < SLOTS - 2:
+                gather_plain(picked_rows[1][:, t, :], 1, t, HALF, S)
+            if t == 0:
+                nc.vector.quantize_mx(out=codes0[:].bitcast(FP8X4), scales=scales0[:], in_=woven0[:])
+        gather_and_weave(woven1_high[:], 1, SLOTS - 2)
         for c in range(CHUNKS):
             multiply(0, c, codes0[:, c * CHUNK : (c + 1) * CHUNK], scales0[:, c * CHUNK : (c + 1) * CHUNK])
 

@@ -31,7 +31,7 @@ CHUNK = 256
 CHUNKS = S // CHUNK
 HALF = S // 2
 DIRECT = [384, 512]
-GPSIMD_WEAVES = [512, 320]
+GPSIMD_WEAVES = [512, 384]
 
 
 def tile_picked_zeropt_none_l_kernel(tc, xT, zp, csum, w1_words, w1_scales, offs, out):
@@ -45,34 +45,30 @@ def tile_picked_zeropt_none_l_kernel(tc, xT, zp, csum, w1_words, w1_scales, offs
         offsets = keep.tile([P, S // ENTRIES_PER_COLUMN], U16, name="offsets")
         nc.sync.dma_start(offsets[:], offs)
 
-        w_scales = [keep.tile([P, N], U8, name=f"w_scales_{z}", align_bytes=64) for z in range(PASSES)]
-        for z in range(PASSES):
-            nc.gpsimd.memset(w_scales[z][:].bitcast(I32), 0)
+        w_scales = keep.tile([P, PASSES * N], U8, name="w_scales", align_bytes=64)
+        nc.gpsimd.memset(w_scales[:].bitcast(I32), 0)
         ident = keep.tile([P, P], F32, name="ident")
         make_identity(nc, ident[:])
         csum_rows = keep.tile([P, P], F32, name="csum_rows")
         nc.gpsimd.memset(csum_rows[:], 0.0)
+        scale_rows = w1_scales.bitcast(I32).rearrange("z r n -> r z n")
+        for q in range(P // 32):
+            nc.gpsimd.dma_start(
+                w_scales[32 * q : 32 * q + SCALE_ROWS, :].bitcast(I32).rearrange("r (z n) -> r z n", z=PASSES),
+                scale_rows[SCALE_ROWS * q : SCALE_ROWS * (q + 1)],
+            )
         w_words = [keep.tile([P, N], U32, name=f"w_words_{z}", align_bytes=64) for z in range(PASSES)]
-
-        def load_weights(z):
-            for q in range(P // 32):
-                nc.sync.dma_start(
-                    w_scales[z][32 * q : 32 * q + SCALE_ROWS, :].bitcast(I32),
-                    w1_scales[z, SCALE_ROWS * q : SCALE_ROWS * (q + 1), :].bitcast(I32),
-                )
-            nc.sync.dma_start(w_words[z][:].bitcast(I32), w1_words[z].rearrange("p n t -> p (n t)").bitcast(I32))
 
         x_rows = xT.rearrange("(z p t) n -> z t p n", z=PASSES, p=P, t=SLOTS)
         planes = {}
         for z in range(PASSES):
             for t in range(SLOTS):
-                if (z, t) == (PASSES - 1, SLOTS - 1):
-                    load_weights(0)
                 planes[z, t] = keep.tile([P, T], F32, name=f"plane_{z}_{t}")
                 nc.sync.dma_start(planes[z, t][:], x_rows[z, t])
                 if (z, t) == (0, 0):
                     nc.sync.dma_start(csum_rows[0:BLOCKS, :], csum.rearrange("(b p) o -> b (p o)", p=P))
-        load_weights(1)
+        for z in range(PASSES):
+            nc.sync.dma_start(w_words[z][:].bitcast(I32), w1_words[z].rearrange("p n t -> p (n t)").bitcast(I32))
 
         def entries(lo, hi):
             return offsets[:, lo // ENTRIES_PER_COLUMN : hi // ENTRIES_PER_COLUMN]
@@ -87,19 +83,19 @@ def tile_picked_zeropt_none_l_kernel(tc, xT, zp, csum, w1_words, w1_scales, offs
                 nc.tensor.transpose(spread[:, i, :], column.to_broadcast([P, P]), ident[:])
             copy = nc.vector.tensor_copy if bank % 2 == 0 else nc.scalar.copy
             copy(zp_view[:, :, first_m : first_m + SPREADS_PER_BANK], spread[:].rearrange("p i n -> p n i"))
-        zp_low = [
-            keep.tile([P, CHUNK], F32, name=f"zp_low_{c}", tag=f"zp_then_codes_{c}", align_bytes=64) for c in range(2)
-        ]
-        zp_high = keep.tile([P, HALF], F32, name="zp_high")
-        zp_picked = [zp_low[0][:], zp_low[1][:], zp_high[:, 0:CHUNK], zp_high[:, CHUNK:HALF]]
-        for c in range(CHUNKS - 1):
-            nc.vector.tensor_copy(zp_picked[c], zp_window[:].indirect(entries(c * CHUNK, (c + 1) * CHUNK)))
-        nc.scalar.activation(zp_picked[CHUNKS - 1], zp_window[:].indirect(entries(S - CHUNK, S)), COPY)
+        zp_picked = keep.tile([P, S], F32, name="zp_picked")
+        nc.vector.tensor_copy(zp_picked[:, 0 : S - CHUNK], zp_window[:].indirect(entries(0, S - CHUNK)))
+        nc.scalar.activation(zp_picked[:, S - CHUNK : S], zp_window[:].indirect(entries(S - CHUNK, S)), COPY)
 
         csum_cols = psum.tile([P, P], F32, name="csum_cols", tag="bank_4")
         nc.tensor.transpose(csum_cols[:], csum_rows[:], ident[:])
         neg_csum = keep.tile([P, BLOCKS], F32, name="neg_csum")
         nc.scalar.activation(neg_csum[:], csum_cols[:, 0:BLOCKS], COPY, scale=-1.0)
+        first_corrections = []
+        for b in range(BLOCKS):
+            correction = keep.tile([P, CHUNK], F32, name=f"correction_{b}", tag=f"correction_then_codes_{b}", align_bytes=64)
+            nc.gpsimd.tensor_scalar(correction[:], zp_picked[:, 0:CHUNK], neg_csum[:, b : b + 1], 0.0, MULT, ADD)
+            first_corrections.append(correction)
 
         picked0 = keep.tile([P, SLOTS * (S - DIRECT[0])], BF16, name="picked0", tag="zp_rows_then_picked0")
         picked1 = keep.tile([P, SLOTS * (S - DIRECT[1])], BF16, name="picked1")
@@ -121,23 +117,23 @@ def tile_picked_zeropt_none_l_kernel(tc, xT, zp, csum, w1_words, w1_scales, offs
         def gather_and_weave(woven, z, t):
             first = DIRECT[z]
             cut = GPSIMD_WEAVES[z]
-            for copy, lo, hi in ((gpsimd_copy, 0, cut), (nc.scalar.copy, cut, S - first)):
+            shares = ((gpsimd_copy, 0, cut // 2), (gpsimd_copy, cut // 2, cut), (nc.scalar.copy, cut, S - first))
+            for copy, lo, hi in shares:
                 gather_plain(picked_rows[z][:, t, lo:hi], z, t, first + lo, first + hi)
-            for copy, lo, hi in ((gpsimd_copy, 0, cut), (nc.scalar.copy, cut, S - first)):
+            for copy, lo, hi in shares:
                 copy(slots(woven)[:, lo:hi, :], picked_rows[z][:, :, lo:hi].rearrange("p t s -> p s t"))
 
         sums = {}
-        for c in range(CHUNKS):
-            for b in range(BLOCKS):
-                sums[c, b] = psum.tile([P, CHUNK], F32, name=f"sums_{c}_{b}", tag=f"bank_{BLOCKS * c + b}")
 
         def multiply(z, c, codes, scales):
             for b in range(BLOCKS):
+                if z == 0:
+                    sums[c, b] = psum.tile([P, CHUNK], F32, name=f"sums_{c}_{b}", tag=f"bank_{BLOCKS * (c % 2) + b}")
                 channels = slice(b * P, (b + 1) * P)
                 nc.tensor.matmul_mx(
                     out=sums[c, b][:],
                     lhsT=w_words[z][:, channels].bitcast(FP8X4),
-                    lhsT_scale=w_scales[z][:, channels],
+                    lhsT_scale=w_scales[:, z * N + b * P : z * N + (b + 1) * P],
                     rhs=codes.bitcast(FP8X4),
                     rhs_scale=scales,
                     start=(z == 0),
@@ -164,8 +160,12 @@ def tile_picked_zeropt_none_l_kernel(tc, xT, zp, csum, w1_words, w1_scales, offs
             if t == 0:
                 nc.vector.quantize_mx(out=codes0[:].bitcast(FP8X4), scales=scales0[:], in_=woven0[:])
         gather_and_weave(woven1_high[:], 1, SLOTS - 2)
-        for c in range(CHUNKS):
+
+        def open_sums(c):
             multiply(0, c, codes0[:, c * CHUNK : (c + 1) * CHUNK], scales0[:, c * CHUNK : (c + 1) * CHUNK])
+
+        open_sums(0)
+        open_sums(1)
 
         last = SLOTS - 1
         last_picked = keep.tile([P, S - CHUNK], BF16, name="last_picked")
@@ -175,38 +175,53 @@ def tile_picked_zeropt_none_l_kernel(tc, xT, zp, csum, w1_words, w1_scales, offs
         def place(copy, c):
             copy(slots(woven1[c])[:, :, last], last_picked[:, (c - 1) * CHUNK : c * CHUNK])
 
-        def finish(c):
+        codes1 = {}
+
+        def quantise_last(c):
             lo, hi = c * CHUNK, (c + 1) * CHUNK
             if hi <= HALF:
                 codes = codes1_low[:, lo:hi]
             else:
-                codes = keep.tile([P, CHUNK], U32, name=f"codes1_{c}", tag=f"zp_then_codes_{c - 2}", align_bytes=64)[:]
+                codes = keep.tile([P, CHUNK], U32, name=f"codes1_{c}", tag=f"correction_then_codes_{c - 2}", align_bytes=64)[:]
             nc.vector.quantize_mx(out=codes.bitcast(FP8X4), scales=scales1[:, lo:hi], in_=woven1[c])
-            multiply(1, c, codes, scales1[:, lo:hi])
+            codes1[c] = codes
+
+        def multiply_last(c):
+            multiply(1, c, codes1[c], scales1[:, c * CHUNK : (c + 1) * CHUNK])
+
+        def finish(c):
+            quantise_last(c)
+            multiply_last(c)
 
         def store(c, b):
             columns = slice(c * CHUNK, (c + 1) * CHUNK)
             result = keep.tile([P, CHUNK], F32, name=f"result_{c}_{b}")
-            nc.vector.scalar_tensor_tensor(
-                result[:], zp_picked[c], neg_csum[:, b : b + 1], sums[c, b][:], MULT, ADD
-            )
+            if c == 0:
+                nc.vector.tensor_tensor(result[:], sums[c, b][:], first_corrections[b][:], ADD)
+            else:
+                nc.vector.scalar_tensor_tensor(
+                    result[:], zp_picked[:, columns], neg_csum[:, b : b + 1], sums[c, b][:], MULT, ADD
+                )
             nc.sync.dma_start(out[b * P : (b + 1) * P, columns], result[:])
 
         gather_direct(woven1[0], 1, last, 0, CHUNK)
         for c in range(1, CHUNKS):
             gather_plain(last_picked[:, (c - 1) * CHUNK : c * CHUNK], 1, last, c * CHUNK, (c + 1) * CHUNK)
         place(nc.vector.tensor_copy, 1)
-        place(nc.scalar.copy, 2)
         place(nc.scalar.copy, 3)
         finish(0)
         finish(1)
+        place(nc.vector.tensor_copy, 2)
         store(0, 0)
         store(0, 1)
+        open_sums(2)
+        quantise_last(2)
+        multiply_last(2)
         store(1, 0)
-        finish(2)
+        quantise_last(3)
         store(1, 1)
-        store(2, 0)
-        finish(3)
-        store(2, 1)
-        store(3, 0)
-        store(3, 1)
+        open_sums(3)
+        multiply_last(3)
+        for c in (2, 3):
+            for b in range(BLOCKS):
+                store(c, b)

@@ -52,11 +52,6 @@ def tile_picked_zeropt_none_l_kernel(tc, xT, zp, csum, w1_words, w1_scales, offs
         csum_rows = keep.tile([P, P], F32, name="csum_rows")
         nc.gpsimd.memset(csum_rows[:], 0.0)
         scale_rows = w1_scales.bitcast(I32).rearrange("z r n -> r z n")
-        for q in range(P // 32):
-            nc.gpsimd.dma_start(
-                w_scales[32 * q : 32 * q + SCALE_ROWS, :].bitcast(I32).rearrange("r (z n) -> r z n", z=PASSES),
-                scale_rows[SCALE_ROWS * q : SCALE_ROWS * (q + 1)],
-            )
         w_words = [keep.tile([P, N], U32, name=f"w_words_{z}", align_bytes=64) for z in range(PASSES)]
 
         x_rows = xT.rearrange("(z p t) n -> z t p n", z=PASSES, p=P, t=SLOTS)
@@ -69,6 +64,12 @@ def tile_picked_zeropt_none_l_kernel(tc, xT, zp, csum, w1_words, w1_scales, offs
                     nc.sync.dma_start(csum_rows[0:BLOCKS, :], csum.rearrange("(b p) o -> b (p o)", p=P))
         for z in range(PASSES):
             nc.sync.dma_start(w_words[z][:].bitcast(I32), w1_words[z].rearrange("p n t -> p (n t)").bitcast(I32))
+            if z == 0:
+                for q in range(P // 32):
+                    nc.sync.dma_start(
+                        w_scales[32 * q : 32 * q + SCALE_ROWS, :].bitcast(I32).rearrange("r (z n) -> r z n", z=PASSES),
+                        scale_rows[SCALE_ROWS * q : SCALE_ROWS * (q + 1)],
+                    )
 
         def entries(lo, hi):
             return offsets[:, lo // ENTRIES_PER_COLUMN : hi // ENTRIES_PER_COLUMN]
@@ -125,9 +126,10 @@ def tile_picked_zeropt_none_l_kernel(tc, xT, zp, csum, w1_words, w1_scales, offs
 
         sums = {}
 
-        def multiply(z, c, codes, scales):
-            for b in range(BLOCKS):
-                if z == 0:
+        def multiply(z, c, codes, scales, blocks=range(BLOCKS)):
+            for b in blocks:
+                opens = (z == 0) != ((c, b) == (1, 1))
+                if opens:
                     sums[c, b] = psum.tile([P, CHUNK], F32, name=f"sums_{c}_{b}", tag=f"bank_{BLOCKS * (c % 2) + b}")
                 channels = slice(b * P, (b + 1) * P)
                 nc.tensor.matmul_mx(
@@ -136,8 +138,8 @@ def tile_picked_zeropt_none_l_kernel(tc, xT, zp, csum, w1_words, w1_scales, offs
                     lhsT_scale=w_scales[:, z * N + b * P : z * N + (b + 1) * P],
                     rhs=codes.bitcast(FP8X4),
                     rhs_scale=scales,
-                    start=(z == 0),
-                    stop=(z == PASSES - 1),
+                    start=opens,
+                    stop=not opens,
                 )
 
         woven0 = keep.tile([P, SLOTS * S], BF16, name="woven0", tag="zp_window_then_pass0", align_bytes=64)
@@ -161,11 +163,11 @@ def tile_picked_zeropt_none_l_kernel(tc, xT, zp, csum, w1_words, w1_scales, offs
                 nc.vector.quantize_mx(out=codes0[:].bitcast(FP8X4), scales=scales0[:], in_=woven0[:])
         gather_and_weave(woven1_high[:], 1, SLOTS - 2)
 
-        def open_sums(c):
-            multiply(0, c, codes0[:, c * CHUNK : (c + 1) * CHUNK], scales0[:, c * CHUNK : (c + 1) * CHUNK])
+        def open_sums(c, blocks=range(BLOCKS)):
+            multiply(0, c, codes0[:, c * CHUNK : (c + 1) * CHUNK], scales0[:, c * CHUNK : (c + 1) * CHUNK], blocks)
 
         open_sums(0)
-        open_sums(1)
+        open_sums(1, [0])
 
         last = SLOTS - 1
         last_picked = keep.tile([P, S - CHUNK], BF16, name="last_picked")
@@ -211,6 +213,7 @@ def tile_picked_zeropt_none_l_kernel(tc, xT, zp, csum, w1_words, w1_scales, offs
         place(nc.scalar.copy, 3)
         finish(0)
         finish(1)
+        open_sums(1, [1])
         place(nc.vector.tensor_copy, 2)
         store(0, 0)
         store(0, 1)

@@ -30,6 +30,7 @@ SPREAD_BANKS = ZP_COLS // SPREADS_PER_BANK
 CHUNK = 256
 CHUNKS = S // CHUNK
 HALF = S // 2
+BANKS = ((0, 1), (2, 3), (0, 5), (1, 2))
 DIRECT = [384, 512]
 GPSIMD_WEAVES = [512, 384]
 
@@ -128,9 +129,9 @@ def tile_picked_zeropt_none_l_kernel(tc, xT, zp, csum, w1_words, w1_scales, offs
 
         def multiply(z, c, codes, scales, blocks=range(BLOCKS)):
             for b in blocks:
-                opens = (z == 0) != ((c, b) == (1, 1))
+                opens = (z == 0) != ((c, b) == (2, 1))
                 if opens:
-                    sums[c, b] = psum.tile([P, CHUNK], F32, name=f"sums_{c}_{b}", tag=f"bank_{BLOCKS * (c % 2) + b}")
+                    sums[c, b] = psum.tile([P, CHUNK], F32, name=f"sums_{c}_{b}", tag=f"bank_{BANKS[c][b]}")
                 channels = slice(b * P, (b + 1) * P)
                 nc.tensor.matmul_mx(
                     out=sums[c, b][:],
@@ -167,7 +168,7 @@ def tile_picked_zeropt_none_l_kernel(tc, xT, zp, csum, w1_words, w1_scales, offs
             multiply(0, c, codes0[:, c * CHUNK : (c + 1) * CHUNK], scales0[:, c * CHUNK : (c + 1) * CHUNK], blocks)
 
         open_sums(0)
-        open_sums(1, [0])
+        open_sums(1)
 
         last = SLOTS - 1
         last_picked = keep.tile([P, S - CHUNK], BF16, name="last_picked")
@@ -198,12 +199,7 @@ def tile_picked_zeropt_none_l_kernel(tc, xT, zp, csum, w1_words, w1_scales, offs
         def store(c, b):
             columns = slice(c * CHUNK, (c + 1) * CHUNK)
             result = keep.tile([P, CHUNK], F32, name=f"result_{c}_{b}")
-            if c == 0:
-                nc.vector.tensor_tensor(result[:], sums[c, b][:], first_corrections[b][:], ADD)
-            else:
-                nc.vector.scalar_tensor_tensor(
-                    result[:], zp_picked[:, columns], neg_csum[:, b : b + 1], sums[c, b][:], MULT, ADD
-                )
+            nc.vector.scalar_tensor_tensor(result[:], zp_picked[:, columns], neg_csum[:, b : b + 1], sums[c, b][:], MULT, ADD)
             nc.sync.dma_start(out[b * P : (b + 1) * P, columns], result[:])
 
         gather_direct(woven1[0], 1, last, 0, CHUNK)
@@ -213,17 +209,20 @@ def tile_picked_zeropt_none_l_kernel(tc, xT, zp, csum, w1_words, w1_scales, offs
         place(nc.scalar.copy, 3)
         finish(0)
         finish(1)
-        open_sums(1, [1])
         place(nc.vector.tensor_copy, 2)
-        store(0, 0)
-        store(0, 1)
-        open_sums(2)
+        first_results = keep.tile([P, BLOCKS, CHUNK], F32, name="first_results")
+        for b in range(BLOCKS):
+            nc.vector.tensor_tensor(first_results[:, b, :], sums[0, b][:], first_corrections[b][:], ADD)
+        nc.sync.dma_start(out.rearrange("(b p) s -> p b s", p=P)[:, :, 0:CHUNK], first_results[:])
+        open_sums(2, [0])
         quantise_last(2)
         multiply_last(2)
+        open_sums(2, [1])
+        open_sums(3, [0])
         store(1, 0)
+        open_sums(3, [1])
         quantise_last(3)
         store(1, 1)
-        open_sums(3)
         multiply_last(3)
         for c in (2, 3):
             for b in range(BLOCKS):

from contextlib import ExitStack

import concourse.mybir as mybir
from concourse.masks import make_identity

K, T, S, N = 1024, 2048, 1024, 256
FLOPS = 2 * K * S * N
BYTES = 4 * K * T + 4 * T + 4 * N + K * N + K * N // 32 + 2 * 128 * S // 16 + 4 * N * S

F32 = mybir.dt.float32
BF16 = mybir.dt.bfloat16
U32 = mybir.dt.uint32
I32 = mybir.dt.int32
U16 = mybir.dt.uint16
U8 = mybir.dt.uint8
FP8X4 = mybir.dt.float8_e4m3fn_x4
MULT = mybir.AluOpType.mult
ADD = mybir.AluOpType.add
COPY = mybir.ActivationFunctionType.Copy

P = 128
SLOTS = 4
PASSES = K // (SLOTS * P)
BLOCKS = N // P
ENTRIES_PER_COLUMN = 16
SCALE_ROWS = 4
ZP_COLS = T // P
SPREADS_PER_BANK = 4
SPREAD_BANKS = ZP_COLS // SPREADS_PER_BANK
CHUNK = 256
CHUNKS = S // CHUNK
HALF = S // 2
BANKS = ((0, 1), (2, 3), (0, 5), (1, 2))
DIRECT = [384, 512]
GPSIMD_WEAVES = [512, 384]


def tile_picked_zeropt_none_l_kernel(tc, xT, zp, csum, w1_words, w1_scales, offs, out):
    nc = tc.nc
    with ExitStack() as ctx:
        keep = ctx.enter_context(tc.tile_pool(name="keep", bufs=1))
        psum = ctx.enter_context(tc.psum_pool(name="psum", bufs=1))

        zp_rows = keep.tile([P, ZP_COLS], F32, name="zp_rows", tag="zp_rows_then_picked0")
        nc.sync.dma_start(zp_rows[:], zp[0, :].rearrange("(n m) -> n m", m=ZP_COLS))
        offsets = keep.tile([P, S // ENTRIES_PER_COLUMN], U16, name="offsets")
        nc.sync.dma_start(offsets[:], offs)

        w_scales = keep.tile([P, PASSES * N], U8, name="w_scales", align_bytes=64)
        nc.gpsimd.memset(w_scales[:].bitcast(I32), 0)
        ident = keep.tile([P, P], F32, name="ident")
        make_identity(nc, ident[:])
        csum_rows = keep.tile([P, P], F32, name="csum_rows")
        nc.gpsimd.memset(csum_rows[:], 0.0)
        scale_rows = w1_scales.bitcast(I32).rearrange("z r n -> r z n")
        w_words = [keep.tile([P, N], U32, name=f"w_words_{z}", align_bytes=64) for z in range(PASSES)]

        x_rows = xT.rearrange("(z p t) n -> z t p n", z=PASSES, p=P, t=SLOTS)
        planes = {}
        for z in range(PASSES):
            for t in range(SLOTS):
                planes[z, t] = keep.tile([P, T], F32, name=f"plane_{z}_{t}")
                nc.sync.dma_start(planes[z, t][:], x_rows[z, t])
                if (z, t) == (0, 0):
                    nc.sync.dma_start(csum_rows[0:BLOCKS, :], csum.rearrange("(b p) o -> b (p o)", p=P))
        for z in range(PASSES):
            nc.sync.dma_start(w_words[z][:].bitcast(I32), w1_words[z].rearrange("p n t -> p (n t)").bitcast(I32))
            if z == 0:
                for q in range(P // 32):
                    nc.sync.dma_start(
                        w_scales[32 * q : 32 * q + SCALE_ROWS, :].bitcast(I32).rearrange("r (z n) -> r z n", z=PASSES),
                        scale_rows[SCALE_ROWS * q : SCALE_ROWS * (q + 1)],
                    )

        def entries(lo, hi):
            return offsets[:, lo // ENTRIES_PER_COLUMN : hi // ENTRIES_PER_COLUMN]

        zp_window = keep.tile([P, T], F32, name="zp_window", tag="zp_window_then_pass0", align_bytes=64)
        zp_view = zp_window[:].rearrange("p (n m) -> p n m", m=ZP_COLS)
        for bank in range(SPREAD_BANKS):
            spread = psum.tile([P, SPREADS_PER_BANK, P], F32, name=f"spread_{bank}", tag=f"bank_{bank}")
            first_m = SPREADS_PER_BANK * bank
            for i in range(SPREADS_PER_BANK):
                column = zp_rows[:, first_m + i : first_m + i + 1]
                nc.tensor.transpose(spread[:, i, :], column.to_broadcast([P, P]), ident[:])
            copy = nc.vector.tensor_copy if bank % 2 == 0 else nc.scalar.copy
            copy(zp_view[:, :, first_m : first_m + SPREADS_PER_BANK], spread[:].rearrange("p i n -> p n i"))
        zp_picked = keep.tile([P, S], F32, name="zp_picked")
        nc.vector.tensor_copy(zp_picked[:, 0 : S - CHUNK], zp_window[:].indirect(entries(0, S - CHUNK)))
        nc.scalar.activation(zp_picked[:, S - CHUNK : S], zp_window[:].indirect(entries(S - CHUNK, S)), COPY)

        csum_cols = psum.tile([P, P], F32, name="csum_cols", tag="bank_4")
        nc.tensor.transpose(csum_cols[:], csum_rows[:], ident[:])
        neg_csum = keep.tile([P, BLOCKS], F32, name="neg_csum")
        nc.scalar.activation(neg_csum[:], csum_cols[:, 0:BLOCKS], COPY, scale=-1.0)
        first_corrections = []
        for b in range(BLOCKS):
            correction = keep.tile([P, CHUNK], F32, name=f"correction_{b}", tag=f"correction_then_codes_{b}", align_bytes=64)
            nc.gpsimd.tensor_scalar(correction[:], zp_picked[:, 0:CHUNK], neg_csum[:, b : b + 1], 0.0, MULT, ADD)
            first_corrections.append(correction)

        picked0 = keep.tile([P, SLOTS * (S - DIRECT[0])], BF16, name="picked0", tag="zp_rows_then_picked0")
        picked1 = keep.tile([P, SLOTS * (S - DIRECT[1])], BF16, name="picked1")
        nc.gpsimd.memset(picked1[:, (SLOTS - 1) * (S - DIRECT[1]) :].bitcast(I32), 0)
        picked_rows = [tile[:].rearrange("p (t s) -> p t s", t=SLOTS) for tile in (picked0, picked1)]

        def slots(woven):
            return woven.rearrange("p (s t) -> p s t", t=SLOTS)

        def gather_direct(woven, z, t, lo, hi):
            nc.vector.tensor_copy(slots(woven)[:, :, t], planes[z, t][:].indirect(entries(lo, hi)))

        def gather_plain(target, z, t, lo, hi):
            nc.scalar.activation(target, planes[z, t][:].indirect(entries(lo, hi)), COPY)

        def gpsimd_copy(target, values):
            nc.gpsimd.tensor_scalar(target, values, 1.0, 0.0, MULT, ADD)

        def gather_and_weave(woven, z, t):
            first = DIRECT[z]
            cut = GPSIMD_WEAVES[z]
            shares = ((gpsimd_copy, 0, cut // 2), (gpsimd_copy, cut // 2, cut), (nc.scalar.copy, cut, S - first))
            for copy, lo, hi in shares:
                gather_plain(picked_rows[z][:, t, lo:hi], z, t, first + lo, first + hi)
            for copy, lo, hi in shares:
                copy(slots(woven)[:, lo:hi, :], picked_rows[z][:, :, lo:hi].rearrange("p t s -> p s t"))

        sums = {}

        def multiply(z, c, codes, scales, blocks=range(BLOCKS)):
            for b in blocks:
                opens = (z == 0) != ((c, b) == (2, 1))
                if opens:
                    sums[c, b] = psum.tile([P, CHUNK], F32, name=f"sums_{c}_{b}", tag=f"bank_{BANKS[c][b]}")
                channels = slice(b * P, (b + 1) * P)
                nc.tensor.matmul_mx(
                    out=sums[c, b][:],
                    lhsT=w_words[z][:, channels].bitcast(FP8X4),
                    lhsT_scale=w_scales[:, z * N + b * P : z * N + (b + 1) * P],
                    rhs=codes.bitcast(FP8X4),
                    rhs_scale=scales,
                    start=opens,
                    stop=not opens,
                )

        woven0 = keep.tile([P, SLOTS * S], BF16, name="woven0", tag="zp_window_then_pass0", align_bytes=64)
        codes0 = keep.tile([P, S], U32, name="codes0", align_bytes=64)
        scales0 = keep.tile([P, S], U8, name="scales0", align_bytes=64)

        for t in range(SLOTS):
            gather_direct(woven0[:, 0 : SLOTS * DIRECT[0]], 0, t, 0, DIRECT[0])
            if t < SLOTS - 1:
                gather_plain(picked_rows[0][:, t, :], 0, t, DIRECT[0], S)
        gather_and_weave(woven0[:, SLOTS * DIRECT[0] :], 0, SLOTS - 1)

        woven1_low = keep.tile([P, SLOTS * HALF], BF16, name="woven1_low", align_bytes=64)
        woven1_high = keep.tile([P, SLOTS * HALF], BF16, name="woven1_high", align_bytes=64)
        woven1 = [w[:, u * SLOTS * CHUNK : (u + 1) * SLOTS * CHUNK] for w in (woven1_low, woven1_high) for u in range(2)]
        for t in range(SLOTS - 1):
            gather_direct(woven1_low[:], 1, t, 0, HALF)
            if t < SLOTS - 2:
                gather_plain(picked_rows[1][:, t, :], 1, t, HALF, S)
            if t == 0:
                nc.vector.quantize_mx(out=codes0[:].bitcast(FP8X4), scales=scales0[:], in_=woven0[:])
        gather_and_weave(woven1_high[:], 1, SLOTS - 2)

        def open_sums(c, blocks=range(BLOCKS)):
            multiply(0, c, codes0[:, c * CHUNK : (c + 1) * CHUNK], scales0[:, c * CHUNK : (c + 1) * CHUNK], blocks)

        open_sums(0)
        open_sums(1)

        last = SLOTS - 1
        last_picked = keep.tile([P, S - CHUNK], BF16, name="last_picked")
        codes1_low = keep.tile([P, HALF], U32, name="codes1_low", align_bytes=64)
        scales1 = keep.tile([P, S], U8, name="scales1", align_bytes=64)

        def place(copy, c):
            copy(slots(woven1[c])[:, :, last], last_picked[:, (c - 1) * CHUNK : c * CHUNK])

        codes1 = {}

        def quantise_last(c):
            lo, hi = c * CHUNK, (c + 1) * CHUNK
            if hi <= HALF:
                codes = codes1_low[:, lo:hi]
            else:
                codes = keep.tile([P, CHUNK], U32, name=f"codes1_{c}", tag=f"correction_then_codes_{c - 2}", align_bytes=64)[:]
            nc.vector.quantize_mx(out=codes.bitcast(FP8X4), scales=scales1[:, lo:hi], in_=woven1[c])
            codes1[c] = codes

        def multiply_last(c):
            multiply(1, c, codes1[c], scales1[:, c * CHUNK : (c + 1) * CHUNK])

        def finish(c):
            quantise_last(c)
            multiply_last(c)

        def store(c, b):
            columns = slice(c * CHUNK, (c + 1) * CHUNK)
            result = keep.tile([P, CHUNK], F32, name=f"result_{c}_{b}")
            nc.vector.scalar_tensor_tensor(result[:], zp_picked[:, columns], neg_csum[:, b : b + 1], sums[c, b][:], MULT, ADD)
            nc.sync.dma_start(out[b * P : (b + 1) * P, columns], result[:])

        gather_direct(woven1[0], 1, last, 0, CHUNK)
        for c in range(1, CHUNKS):
            gather_plain(last_picked[:, (c - 1) * CHUNK : c * CHUNK], 1, last, c * CHUNK, (c + 1) * CHUNK)
        place(nc.vector.tensor_copy, 1)
        place(nc.scalar.copy, 3)
        finish(0)
        finish(1)
        place(nc.vector.tensor_copy, 2)
        first_results = keep.tile([P, BLOCKS, CHUNK], F32, name="first_results")
        for b in range(BLOCKS):
            nc.vector.tensor_tensor(first_results[:, b, :], sums[0, b][:], first_corrections[b][:], ADD)
        nc.sync.dma_start(out.rearrange("(b p) s -> p b s", p=P)[:, :, 0:CHUNK], first_results[:])
        open_sums(2, [0])
        quantise_last(2)
        multiply_last(2)
        open_sums(2, [1])
        open_sums(3, [0])
        store(1, 0)
        open_sums(3, [1])
        quantise_last(3)
        store(1, 1)
        multiply_last(3)
        for c in (2, 3):
            for b in range(BLOCKS):
                store(c, b)
